import numpy as np
import ml_dtypes


def mxq(x, axis, fmt="e4m3"):
    dtype, down = {"e4m3": (ml_dtypes.float8_e4m3fn, 7), "e5m2": (ml_dtypes.float8_e5m2, 14)}[fmt]
    v = np.moveaxis(np.asarray(x, np.float32).astype(ml_dtypes.bfloat16).astype(np.float64), axis, -1)
    blocks = v.reshape(v.shape[:-1] + (-1, 32))
    amax = np.abs(blocks).max(-1, keepdims=True)
    byte = np.maximum(np.where(amax > 0, np.frexp(amax)[1] - 1 + 127, 0) - down, 1)
    scale = np.exp2(byte - 127.0)
    codes = (blocks / scale).astype(np.float32).astype(dtype).astype(np.float64)
    return np.moveaxis((codes * scale).reshape(v.shape), -1, axis)


WIDE = False


def mx_kscale(k):
    if not WIDE:
        return np.ones(k)
    levels = np.array([10, -10, 5, -5, 0])
    if k % 512:
        return np.exp2(np.random.permutation(np.resize(levels, k // 32))).repeat(32)
    a = np.empty((k // 512, 16))
    for p in range(k // 512):
        a[p, :8] = np.random.permutation(np.resize(levels, 8))
        for g in range(8):
            far = levels[np.abs(levels - a[p, g]) >= 10]
            a[p, g + 8] = far[np.random.randint(len(far))]
    return np.exp2(a.ravel()).repeat(32)


def f64(x):
    return np.asarray(x).astype(np.float64)


def striped(idx):
    return np.tile(idx.reshape(-1, 16).T, (8, 1)).astype(np.uint16)


def unstriped(offs):
    return offs[:16].T.reshape(-1).astype(np.int64)


def d_relu(v):
    return (v > 0).astype(np.float64)


K, T, E, C, H, N = 256, 2560, 2, 1024, 256, 512


def by_expert(wq, xq):
    return np.concatenate([wq[e].T @ xq[:, e * C:(e + 1) * C] for e in range(E)], axis=1)


def setup_inputs():
    n = np.random.standard_normal
    slot_token = np.random.permutation(T)[:E * C]
    s = mx_kscale(N)[:, None]
    z = np.ones(T); z[slot_token] = mx_kscale(E * C)
    return {
        "xT": (n((K, T)) * z[None, :]).astype(np.float32),
        "dyT": (n((N, T)) * s).astype(np.float32),
        "a": n((H, E * C)).astype(np.float32),
        "w2": (n((E, N, H)) / np.sqrt(N) / s[None]).astype(np.float32),
        "gate": np.tile(np.random.uniform(0.2, 1.0, E * C) / z[slot_token], (N, 1)).astype(np.float32),
        "offs": striped(slot_token),
    }


def reference(xT, dyT, a, w2, gate, offs):
    idx = unstriped(offs)
    gq = mxq(f64(gate) * f64(dyT)[:, idx], 0, "e4m3")
    dh = by_expert(mxq(f64(w2), 1, "e4m3"), gq)
    da = mxq(dh * d_relu(f64(a)), 1, "e4m3")
    xq = mxq(f64(xT)[:, idx], 1, "e4m3")
    return np.stack([(xq[:, e * C:(e + 1) * C] @ da[:, e * C:(e + 1) * C].T) for e in range(E)])

@@ -1,0 +1,163 @@
+from contextlib import ExitStack
+
+import concourse.mybir as mybir
+from concourse.masks import make_identity
+
+K, T, E, C, H, N = 256, 2560, 2, 1024, 256, 512
+FLOPS = 2 * E * C * (N * H + K * H)
+BYTES = 4 * (K * T + N * T + H * E * C + E * N * H + E * C + E * K * H) + 2 * 128 * 128
+
+F32 = mybir.dt.float32
+BF16 = mybir.dt.bfloat16
+U32 = mybir.dt.uint32
+U16 = mybir.dt.uint16
+U8 = mybir.dt.uint8
+FP8X4 = mybir.dt.float8_e4m3fn_x4
+ALU = mybir.AluOpType
+
+P = 128
+PACK = 4
+PASS = P * PACK
+PASSES = E * C // PASS
+LIST_COLS = PASS // 16
+X_CUTS = [0,640,1280,1920,2560]
+LOADS = "d0 d1 x0 x1 d2 x2 x3 w0 d3 w1 a0 a1 a2 a3".split()
+STEPS = "D00 D01 D02 D03 F10 P0 P1 P2 P3 F20 W0 D30 I0 D31 I1 X0 X1 Qw0 D32 I2 D33 W1 I3 Qg0 S0 do0 xo0 xo1 Qg1 S1 do1 Qw1 Qg2 X2 xo2 S2 do2 Qd0 Qx0 m0 Qg3 X3 xo3 Qd1 Qx1 m1 S3 do3 Qd2 Qx2 m2 Qx3 Qd3 m3".split()
+
+
+def tile_moe_mlp_relu_kernel(tc, xT, dyT, a, w2, gate, offs, out):
+    nc = tc.nc
+    with ExitStack() as ctx:
+        keep = ctx.enter_context(tc.tile_pool(name="keep", bufs=1))
+        psum = ctx.enter_context(tc.psum_pool(name="psum", bufs=1))
+
+        offsets = keep.tile([P, E * C // 16], U16, name="offsets")
+
+        gate_cols = keep.tile([P, PASSES, 8], F32, name="gate_cols")
+        nc.sync.dma_start(gate_cols[:, :, 0:PACK], gate[0].rearrange("(c p i) -> p c i", c=PASSES, i=PACK))
+        nc.sync.dma_start(offsets[:], offs)
+
+        ident = keep.tile([P, P], F32, name="ident")
+        make_identity(nc, ident[:])
+
+        dy_rows = dyT.rearrange("(p j) t -> j p t", j=PACK)
+        dy = [keep.tile([P, T], F32, name=f"dy{j}") for j in range(PACK)]
+        x_rows = xT.rearrange("(p e) t -> p e t", e=2)
+        x_raw = [keep.tile([P, 2, X_CUTS[q + 1] - X_CUTS[q]], F32, name=f"x_raw{q}") for q in range(len(X_CUTS) - 1)]
+        w_raw = [keep.tile([P, PACK, H], F32, name=f"w_raw{e}") for e in range(E)]
+        a_rows = a.rearrange("(h p) s -> p h s", p=P)
+        a_sb = [keep.tile([P, 2, PASS], F32, name=f"a_sb{c}") for c in range(PASSES)]
+
+        for name in LOADS:
+            n = int(name[1:])
+            if name[0] == "d":
+                nc.sync.dma_start(dy[n][:], dy_rows[n])
+            elif name[0] == "x":
+                nc.sync.dma_start(x_raw[n][:], x_rows[:, :, X_CUTS[n]:X_CUTS[n + 1]])
+            elif name[0] == "w":
+                nc.sync.dma_start(w_raw[n][:], w2[n].rearrange("(p j) i -> p j i", j=PACK))
+            else:
+                nc.sync.dma_start(a_sb[n][:], a_rows[:, :, n * PASS:(n + 1) * PASS])
+
+        def quantize(src, name):
+            width = src.shape[1]
+            codes = keep.tile([P, width], U32, name=name + "_codes", align_bytes=64)
+            scales = keep.tile([P, width], U8, name=name + "_scales", align_bytes=64)
+            nc.vector.quantize_mx(out=codes[:].bitcast(FP8X4), scales=scales[:], in_=src[:].rearrange("p w j -> p (w j)"))
+            return codes, scales
+
+        def turned_bank():
+            return psum.tile([P, PACK, P], F32, name="turned", tag="turned", bufs=3)
+
+        gate_sb = keep.tile([P, E * C], F32, name="gate_sb")
+        for c in range(PASSES):
+            bank = turned_bank()
+            for i in range(PACK):
+                nc.tensor.transpose(bank[:, i, :], gate_cols[:, c, i:i + 1].to_broadcast([P, P]), ident[:])
+            nc.scalar.copy(gate_sb[:, c * PASS:(c + 1) * PASS].rearrange("q (p i) -> q p i", i=PACK), bank[:].rearrange("q i p -> q p i"))
+
+        g32 = keep.tile([P, PACK, E * C], F32, name="g32")
+
+        def g_part(c, n):
+            return g32[:, :, c * PASS:(c + n) * PASS]
+
+        def gather_dy(j, c, n):
+            nc.vector.tensor_tensor(g_part(c, n)[:, j, :], dy[j][:].indirect(offsets[:, c * LIST_COLS:(c + n) * LIST_COLS]),
+                                    gate_sb[:, c * PASS:(c + n) * PASS], ALU.mult)
+
+        x_pairs = keep.tile([P, T], U32, name="x_pairs")
+        x_pairs_bf = x_pairs[:].bitcast(BF16).rearrange("p (t e) -> p t e", e=2)
+
+        def interleave(dst, src):
+            nc.scalar.copy(dst.rearrange("p (c i) j -> p c j i", i=4), src.rearrange("p j (c i) -> p c j i", i=4))
+
+        w_bf, x_bank, x_bf, g_bf, gq, wq, xq, daq, dh, da_bank, da_turned, acc = {}, {}, {}, {}, {}, {}, {}, {}, {}, {}, {}, {}
+
+        for step in STEPS:
+            op, c = step[:-1], int(step[-1])
+            e = c // 2
+            if op[0] == "D":
+                gather_dy(int(op[1]), c, 1)
+            elif op[0] == "E":
+                gather_dy(int(op[1]), c, 2)
+            elif op[0] == "F":
+                gather_dy(int(op[1]), c, 4)
+            elif op == "P":
+                nc.scalar.copy(x_pairs_bf[:, X_CUTS[c]:X_CUTS[c + 1], :], x_raw[c][:].rearrange("p e t -> p t e"))
+            elif op == "W":
+                w_bf[c] = keep.tile([P, H, PACK], BF16, name=f"w_bf{c}", align_bytes=64)
+                interleave(w_bf[c][:], w_raw[c][:])
+            elif op == "Qw":
+                wq[c] = quantize(w_bf[c], f"w{c}")
+            elif op == "X":
+                xg = keep.tile([P, PASS], U32, name=f"x_slots{c}")
+                nc.vector.tensor_copy(xg[:].rearrange("p (t m) -> p m t", t=PACK), x_pairs[:].indirect(offsets[:, c * LIST_COLS:(c + 1) * LIST_COLS]))
+                x_bank[c] = turned_bank()
+                for t in range(PACK):
+                    nc.tensor.transpose(x_bank[c][:, t, :], xg[:].bitcast(F32)[:, t * P:(t + 1) * P], ident[:])
+            elif op == "xo":
+                x_bf[c] = keep.tile([P, K, PACK], BF16, name=f"x_bf{c}", align_bytes=64)
+                nc.scalar.copy(x_bf[c][:], x_bank[c][:].rearrange("p t k -> p (t k)").bitcast(BF16).rearrange("p (t k) -> p k t", t=PACK))
+            elif op == "Qx":
+                xq[c] = quantize(x_bf[c], f"x{c}")
+            elif op == "I":
+                g_bf[c] = keep.tile([P, PASS, PACK], BF16, name=f"g_bf{c}", align_bytes=64)
+                interleave(g_bf[c][:], g_part(c, 1))
+            elif op == "Qg":
+                gq[c] = quantize(g_bf[c], f"g{c}")
+                for h in range(2):
+                    dh[c, h] = psum.tile([P, PASS], F32, name="dh", tag="dh", bufs=3)
+                    cols = slice(h * P, (h + 1) * P)
+                    nc.tensor.matmul_mx(dh[c, h][:], lhsT=wq[e][0][:, cols].bitcast(FP8X4), lhsT_scale=wq[e][1][:, cols],
+                                        rhs=gq[c][0][:].bitcast(FP8X4), rhs_scale=gq[c][1][:], start=True, stop=True)
+            elif op == "S":
+                da_bank[c] = turned_bank()
+                for h in range(2):
+                    da = keep.tile([P, PASS], BF16, name=f"da{c}_{h}")
+                    nc.vector.scalar_tensor_tensor(da[:], a_sb[c][:, h, :], 0.0, dh[c, h][:], ALU.is_gt, ALU.mult)
+                    for u in range(2):
+                        nc.tensor.transpose(da_bank[c][:, 2 * h + u, :], da[:].bitcast(F32)[:, u:PASS // 2:2], ident[:])
+            elif op == "do":
+                dt = keep.tile([P, H, PACK], BF16, name=f"da_turned{c}", align_bytes=64)
+                nc.scalar.copy(dt[:].rearrange("p i t -> p (i t)").bitcast(F32).rearrange("p (h i u) -> p h i u", h=2, u=2),
+                               da_bank[c][:].rearrange("p (h u) i -> p h i u", u=2))
+                da_turned[c] = dt
+            elif op == "Qd":
+                daq[c] = quantize(da_turned[c], f"da{c}")
+            else:
+                first = c % 2 == 0
+                for h in range(2):
+                    if first:
+                        acc[h] = psum.tile([P, H], F32, name=f"acc{h}", tag=f"acc{h}", bufs=1)
+                    cols = slice(h * P, (h + 1) * P)
+                    nc.tensor.matmul_mx(acc[h][:], lhsT=xq[c][0][:, cols].bitcast(FP8X4), lhsT_scale=xq[c][1][:, cols],
+                                        rhs=daq[c][0][:].bitcast(FP8X4), rhs_scale=daq[c][1][:], start=first, stop=not first)
+                if not first:
+                    for h in range(2):
+                        res = keep.tile([P, H], F32, name=f"res{e}_{h}")
+                        if h == 1 and e == E - 1:
+                            nc.vector.tensor_copy(res[:], acc[h][:])
+                            nc.sync.dma_start(out[e, h * P:(h + 1) * P, :], res[:])
+                        else:
+                            nc.scalar.copy(res[:], acc[h][:])
+                            nc.sync.dma_start(out[e, h * P:(h + 1) * P, :], res[:])

@@ -21,8 +21,8 @@ PASS = P * PACK
 PASSES = E * C // PASS
 LIST_COLS = PASS // 16
 X_CUTS = [0,640,1280,1920,2560]
-LOADS = "d0 d1 x0 x1 d2 x2 x3 w0 d3 w1 a0 a1 a2 a3".split()
-STEPS = "D00 D01 D02 D03 F10 P0 P1 P2 P3 F20 W0 D30 I0 D31 I1 X0 X1 Qw0 D32 I2 D33 W1 I3 Qg0 S0 do0 xo0 xo1 Qg1 S1 do1 Qw1 Qg2 X2 xo2 S2 do2 Qd0 Qx0 m0 Qg3 X3 xo3 Qd1 Qx1 m1 S3 do3 Qd2 Qx2 m2 Qx3 Qd3 m3".split()
+LOADS = "d0 d1 x0 x1 x2 x3 w0 w1 d2 d3 A0 A1".split()
+STEPS = "D00 D01 D02 D03 F10 P0 P1 P2 P3 W0 W1 X0 xo0 X1 xo1 X2 xo2 X3 xo3 D20 D30 I0 D21 D31 I1 D22 D32 I2 D23 Qw0 Qg0 D33 I3 Qg1 S0 do0 Qw1 Qg2 S1 do1 Qg3 S2 do2 S3 do3 Qd0 Qx0 m0 Qd1 Qx1 m1 Qd2 Qx2 m2 Qx3 Qd3 m3".split()
 
 
 def tile_moe_mlp_relu_kernel(tc, xT, dyT, a, w2, gate, offs, out):
@@ -46,7 +46,7 @@ def tile_moe_mlp_relu_kernel(tc, xT, dyT, a, w2, gate, offs, out):
         x_raw = [keep.tile([P, 2, X_CUTS[q + 1] - X_CUTS[q]], F32, name=f"x_raw{q}") for q in range(len(X_CUTS) - 1)]
         w_raw = [keep.tile([P, PACK, H], F32, name=f"w_raw{e}") for e in range(E)]
         a_rows = a.rearrange("(h p) s -> p h s", p=P)
-        a_sb = [keep.tile([P, 2, PASS], F32, name=f"a_sb{c}") for c in range(PASSES)]
+        a_sb = [keep.tile([P, 2, C], F32, name=f"a_sb{e}") for e in range(E)]
 
         for name in LOADS:
             n = int(name[1:])
@@ -57,7 +57,7 @@ def tile_moe_mlp_relu_kernel(tc, xT, dyT, a, w2, gate, offs, out):
             elif name[0] == "w":
                 nc.sync.dma_start(w_raw[n][:], w2[n].rearrange("(p j) i -> p j i", j=PACK))
             else:
-                nc.sync.dma_start(a_sb[n][:], a_rows[:, :, n * PASS:(n + 1) * PASS])
+                nc.sync.dma_start(a_sb[n][:], a_rows[:, :, n * C:(n + 1) * C])
 
         def quantize(src, name):
             width = src.shape[1]
@@ -67,7 +67,7 @@ def tile_moe_mlp_relu_kernel(tc, xT, dyT, a, w2, gate, offs, out):
             return codes, scales
 
         def turned_bank():
-            return psum.tile([P, PACK, P], F32, name="turned", tag="turned", bufs=3)
+            return psum.tile([P, PACK, P], F32, name="turned", tag="turned", bufs=4)
 
         gate_sb = keep.tile([P, E * C], F32, name="gate_sb")
         for c in range(PASSES):
@@ -93,6 +93,11 @@ def tile_moe_mlp_relu_kernel(tc, xT, dyT, a, w2, gate, offs, out):
 
         w_bf, x_bank, x_bf, g_bf, gq, wq, xq, daq, dh, da_bank, da_turned, acc = {}, {}, {}, {}, {}, {}, {}, {}, {}, {}, {}, {}
 
+        def second(dst, c, h):
+            cols = slice(h * P, (h + 1) * P)
+            nc.tensor.matmul_mx(dst, lhsT=xq[c][0][:, cols].bitcast(FP8X4), lhsT_scale=xq[c][1][:, cols],
+                                rhs=daq[c][0][:].bitcast(FP8X4), rhs_scale=daq[c][1][:], start=c % 2 == 0, stop=c % 2 == 1)
+
         for step in STEPS:
             op, c = step[:-1], int(step[-1])
             e = c // 2
@@ -111,10 +116,10 @@ def tile_moe_mlp_relu_kernel(tc, xT, dyT, a, w2, gate, offs, out):
                 wq[c] = quantize(w_bf[c], f"w{c}")
             elif op == "X":
                 xg = keep.tile([P, PASS], U32, name=f"x_slots{c}")
-                nc.vector.tensor_copy(xg[:].rearrange("p (t m) -> p m t", t=PACK), x_pairs[:].indirect(offsets[:, c * LIST_COLS:(c + 1) * LIST_COLS]))
+                nc.vector.tensor_copy(xg[:], x_pairs[:].indirect(offsets[:, c * LIST_COLS:(c + 1) * LIST_COLS]))
                 x_bank[c] = turned_bank()
                 for t in range(PACK):
-                    nc.tensor.transpose(x_bank[c][:, t, :], xg[:].bitcast(F32)[:, t * P:(t + 1) * P], ident[:])
+                    nc.tensor.transpose(x_bank[c][:, t, :], xg[:].bitcast(F32)[:, t:PASS:PACK], ident[:])
             elif op == "xo":
                 x_bf[c] = keep.tile([P, K, PACK], BF16, name=f"x_bf{c}", align_bytes=64)
                 nc.scalar.copy(x_bf[c][:], x_bank[c][:].rearrange("p t k -> p (t k)").bitcast(BF16).rearrange("p (t k) -> p k t", t=PACK))
@@ -126,7 +131,7 @@ def tile_moe_mlp_relu_kernel(tc, xT, dyT, a, w2, gate, offs, out):
             elif op == "Qg":
                 gq[c] = quantize(g_bf[c], f"g{c}")
                 for h in range(2):
-                    dh[c, h] = psum.tile([P, PASS], F32, name="dh", tag="dh", bufs=3)
+                    dh[c, h] = psum.tile([P, PASS], F32, name="dh", tag="dh", bufs=4)
                     cols = slice(h * P, (h + 1) * P)
                     nc.tensor.matmul_mx(dh[c, h][:], lhsT=wq[e][0][:, cols].bitcast(FP8X4), lhsT_scale=wq[e][1][:, cols],
                                         rhs=gq[c][0][:].bitcast(FP8X4), rhs_scale=gq[c][1][:], start=True, stop=True)
@@ -134,7 +139,7 @@ def tile_moe_mlp_relu_kernel(tc, xT, dyT, a, w2, gate, offs, out):
                 da_bank[c] = turned_bank()
                 for h in range(2):
                     da = keep.tile([P, PASS], BF16, name=f"da{c}_{h}")
-                    nc.vector.scalar_tensor_tensor(da[:], a_sb[c][:, h, :], 0.0, dh[c, h][:], ALU.is_gt, ALU.mult)
+                    nc.vector.scalar_tensor_tensor(da[:], a_sb[e][:, h, (c % 2) * PASS:(c % 2 + 1) * PASS], 0.0, dh[c, h][:], ALU.is_gt, ALU.mult)
                     for u in range(2):
                         nc.tensor.transpose(da_bank[c][:, 2 * h + u, :], da[:].bitcast(F32)[:, u:PASS // 2:2], ident[:])
             elif op == "do":
@@ -144,20 +149,26 @@ def tile_moe_mlp_relu_kernel(tc, xT, dyT, a, w2, gate, offs, out):
                 da_turned[c] = dt
             elif op == "Qd":
                 daq[c] = quantize(da_turned[c], f"da{c}")
-            else:
-                first = c % 2 == 0
+            elif c == 1:
+                bank = psum.tile([P, PASS], F32, name="acc0", tag="dh", bufs=4)
                 for h in range(2):
-                    if first:
-                        acc[h] = psum.tile([P, H], F32, name=f"acc{h}", tag=f"acc{h}", bufs=1)
-                    cols = slice(h * P, (h + 1) * P)
-                    nc.tensor.matmul_mx(acc[h][:], lhsT=xq[c][0][:, cols].bitcast(FP8X4), lhsT_scale=xq[c][1][:, cols],
-                                        rhs=daq[c][0][:].bitcast(FP8X4), rhs_scale=daq[c][1][:], start=first, stop=not first)
-                if not first:
-                    for h in range(2):
-                        res = keep.tile([P, H], F32, name=f"res{e}_{h}")
-                        if h == 1 and e == E - 1:
-                            nc.vector.tensor_copy(res[:], acc[h][:])
-                            nc.sync.dma_start(out[e, h * P:(h + 1) * P, :], res[:])
-                        else:
-                            nc.scalar.copy(res[:], acc[h][:])
-                            nc.sync.dma_start(out[e, h * P:(h + 1) * P, :], res[:])
+                    for cc in range(2):
+                        second(bank[:, h * H:(h + 1) * H], cc, h)
+                res = keep.tile([P, 2, H], F32, name="res0")
+                nc.scalar.copy(res[:].rearrange("p h i -> p (h i)"), bank[:])
+                nc.sync.dma_start(out[0].rearrange("(h p) i -> p h i", p=P), res[:])
+            elif c == 2:
+                for h in range(2):
+                    acc[h] = psum.tile([P, PASS], F32, name=f"acc1_{h}", tag="dh", bufs=4)
+                    second(acc[h][:, 0:H], c, h)
+            elif c == 3:
+                for h in range(2):
+                    second(acc[h][:, 0:H], c, h)
+                for h in range(2):
+                    res = keep.tile([P, H], F32, name=f"res1_{h}")
+                    if h == 1:
+                        nc.vector.tensor_copy(res[:], acc[h][:, 0:H])
+                        nc.sync.dma_start(out[1, h * P:(h + 1) * P, :], res[:])
+                    else:
+                        nc.scalar.copy(res[:], acc[h][:, 0:H])
+                        nc.sync.dma_start(out[1, h * P:(h + 1) * P, :], res[:])

@@ -21,8 +21,9 @@ PASS = P * PACK
 PASSES = E * C // PASS
 LIST_COLS = PASS // 16
 X_CUTS = [0,640,1280,1920,2560]
-LOADS = "d0 d1 x0 x1 x2 x3 w0 w1 d2 d3 A0 A1".split()
-STEPS = "D00 D01 D02 D03 F10 P0 P1 P2 P3 W0 W1 X0 xo0 X1 xo1 X2 xo2 X3 xo3 D20 D30 I0 D21 D31 I1 D22 D32 I2 D23 Qw0 Qg0 D33 I3 Qg1 S0 do0 Qw1 Qg2 S1 do1 Qg3 S2 do2 S3 do3 Qd0 Qx0 m0 Qd1 Qx1 m1 Qd2 Qx2 m2 Qx3 Qd3 m3".split()
+DY_CUT = 2304
+LOADS = "d0 d1 x0 x1 x2 x3 w0 w1 dA d3 dB A0 A1".split()
+STEPS = "D00 D01 D02 D03 D10 D11 D12 D13 P0 P1 P2 P3 W0 W1 X0 xo0 X1 xo1 X2 xo2 X3 xo3 Qw0 Qw1 D30 D20 I0 D31 D21 I1 D32 D22 I2 Qg0 D33 D23 I3 Qg1 S0 Qg2 S1 Qg3 S2 S3 do0 do1 do2 do3 Qd0 Qx0 m0 Qd1 Qx1 m1 Qd2 Qx2 m2 Qx3 Qd3 m3".split()
 
 
 def tile_moe_mlp_relu_kernel(tc, xT, dyT, a, w2, gate, offs, out):
@@ -46,11 +47,15 @@ def tile_moe_mlp_relu_kernel(tc, xT, dyT, a, w2, gate, offs, out):
         x_raw = [keep.tile([P, 2, X_CUTS[q + 1] - X_CUTS[q]], F32, name=f"x_raw{q}") for q in range(len(X_CUTS) - 1)]
         w_raw = [keep.tile([P, PACK, H], F32, name=f"w_raw{e}") for e in range(E)]
         a_rows = a.rearrange("(h p) s -> p h s", p=P)
-        a_sb = [keep.tile([P, 2, C], F32, name=f"a_sb{e}") for e in range(E)]
+        a_sb = [keep.tile([P, 2, C], F32, name=f"a_sb{e}", tag=f"a_sb{e}", align_bytes=64) for e in range(E)]
 
         for name in LOADS:
-            n = int(name[1:])
-            if name[0] == "d":
+            n = int(name[1:], 16)
+            if name == "dA":
+                nc.sync.dma_start(dy[2][:, :DY_CUT], dy_rows[2][:, :DY_CUT])
+            elif name == "dB":
+                nc.sync.dma_start(dy[2][:, DY_CUT:], dy_rows[2][:, DY_CUT:])
+            elif name[0] == "d":
                 nc.sync.dma_start(dy[n][:], dy_rows[n])
             elif name[0] == "x":
                 nc.sync.dma_start(x_raw[n][:], x_rows[:, :, X_CUTS[n]:X_CUTS[n + 1]])
@@ -59,44 +64,45 @@ def tile_moe_mlp_relu_kernel(tc, xT, dyT, a, w2, gate, offs, out):
             else:
                 nc.sync.dma_start(a_sb[n][:], a_rows[:, :, n * C:(n + 1) * C])
 
-        def quantize(src, name):
+        def quantize(src, name, codes=None):
             width = src.shape[1]
-            codes = keep.tile([P, width], U32, name=name + "_codes", align_bytes=64)
+            if codes is None:
+                codes = keep.tile([P, width], U32, name=name + "_codes", align_bytes=64)[:]
             scales = keep.tile([P, width], U8, name=name + "_scales", align_bytes=64)
-            nc.vector.quantize_mx(out=codes[:].bitcast(FP8X4), scales=scales[:], in_=src[:].rearrange("p w j -> p (w j)"))
+            nc.vector.quantize_mx(out=codes.bitcast(FP8X4), scales=scales[:], in_=src[:].rearrange("p w j -> p (w j)"))
             return codes, scales
 
         def turned_bank():
             return psum.tile([P, PACK, P], F32, name="turned", tag="turned", bufs=4)
 
-        gate_sb = keep.tile([P, E * C], F32, name="gate_sb")
+        gate_sb = [keep.tile([P, PASS], F32, name=f"gate_sb{c}") for c in range(PASSES)]
         for c in range(PASSES):
             bank = turned_bank()
             for i in range(PACK):
                 nc.tensor.transpose(bank[:, i, :], gate_cols[:, c, i:i + 1].to_broadcast([P, P]), ident[:])
-            nc.scalar.copy(gate_sb[:, c * PASS:(c + 1) * PASS].rearrange("q (p i) -> q p i", i=PACK), bank[:].rearrange("q i p -> q p i"))
+            nc.scalar.copy(gate_sb[c][:].rearrange("q (p i) -> q p i", i=PACK), bank[:].rearrange("q i p -> q p i"))
 
-        g32 = keep.tile([P, PACK, E * C], F32, name="g32")
+        g32 = [keep.tile([P, PACK, PASS], F32, name=f"g32_{c}", tag=f"g32_{c}") for c in range(PASSES)]
 
         def g_part(c, n):
-            return g32[:, :, c * PASS:(c + n) * PASS]
+            return g32[c][:]
 
         def gather_dy(j, c, n):
             nc.vector.tensor_tensor(g_part(c, n)[:, j, :], dy[j][:].indirect(offsets[:, c * LIST_COLS:(c + n) * LIST_COLS]),
-                                    gate_sb[:, c * PASS:(c + n) * PASS], ALU.mult)
+                                    gate_sb[c][:], ALU.mult)
 
         x_pairs = keep.tile([P, T], U32, name="x_pairs")
         x_pairs_bf = x_pairs[:].bitcast(BF16).rearrange("p (t e) -> p t e", e=2)
 
         def interleave(dst, src):
-            nc.scalar.copy(dst.rearrange("p (c i) j -> p c j i", i=4), src.rearrange("p j (c i) -> p c j i", i=4))
+            nc.scalar.copy(dst.rearrange("p (c i) j -> p c j i", i=2), src.rearrange("p j (c i) -> p c j i", i=2))
 
         w_bf, x_bank, x_bf, g_bf, gq, wq, xq, daq, dh, da_bank, da_turned, acc = {}, {}, {}, {}, {}, {}, {}, {}, {}, {}, {}, {}
 
         def second(dst, c, h):
             cols = slice(h * P, (h + 1) * P)
             nc.tensor.matmul_mx(dst, lhsT=xq[c][0][:, cols].bitcast(FP8X4), lhsT_scale=xq[c][1][:, cols],
-                                rhs=daq[c][0][:].bitcast(FP8X4), rhs_scale=daq[c][1][:], start=c % 2 == 0, stop=c % 2 == 1)
+                                rhs=daq[c][0].bitcast(FP8X4), rhs_scale=daq[c][1][:], start=c % 2 == 0, stop=c % 2 == 1)
 
         for step in STEPS:
             op, c = step[:-1], int(step[-1])
@@ -124,7 +130,9 @@ def tile_moe_mlp_relu_kernel(tc, xT, dyT, a, w2, gate, offs, out):
                 x_bf[c] = keep.tile([P, K, PACK], BF16, name=f"x_bf{c}", align_bytes=64)
                 nc.scalar.copy(x_bf[c][:], x_bank[c][:].rearrange("p t k -> p (t k)").bitcast(BF16).rearrange("p (t k) -> p k t", t=PACK))
             elif op == "Qx":
-                xq[c] = quantize(x_bf[c], f"x{c}")
+                if c == 0:
+                    x_codes = keep.tile([P, PASSES, K], U32, name="x_codes", tag="a_sb1", align_bytes=64)
+                xq[c] = quantize(x_bf[c], f"x{c}", x_codes[:, c, :])
             elif op == "I":
                 g_bf[c] = keep.tile([P, PASS, PACK], BF16, name=f"g_bf{c}", align_bytes=64)
                 interleave(g_bf[c][:], g_part(c, 1))
@@ -134,14 +142,15 @@ def tile_moe_mlp_relu_kernel(tc, xT, dyT, a, w2, gate, offs, out):
                     dh[c, h] = psum.tile([P, PASS], F32, name="dh", tag="dh", bufs=4)
                     cols = slice(h * P, (h + 1) * P)
                     nc.tensor.matmul_mx(dh[c, h][:], lhsT=wq[e][0][:, cols].bitcast(FP8X4), lhsT_scale=wq[e][1][:, cols],
-                                        rhs=gq[c][0][:].bitcast(FP8X4), rhs_scale=gq[c][1][:], start=True, stop=True)
+                                        rhs=gq[c][0].bitcast(FP8X4), rhs_scale=gq[c][1][:], start=True, stop=True)
             elif op == "S":
                 da_bank[c] = turned_bank()
+                da_both = keep.tile([P, 2, PASS], BF16, name=f"da{c}", tag=f"g32_{(c + 1) % PASSES}")
                 for h in range(2):
-                    da = keep.tile([P, PASS], BF16, name=f"da{c}_{h}")
-                    nc.vector.scalar_tensor_tensor(da[:], a_sb[e][:, h, (c % 2) * PASS:(c % 2 + 1) * PASS], 0.0, dh[c, h][:], ALU.is_gt, ALU.mult)
+                    da = da_both[:, h, :]
+                    nc.vector.scalar_tensor_tensor(da, a_sb[e][:, h, (c % 2) * PASS:(c % 2 + 1) * PASS], 0.0, dh[c, h][:], ALU.is_gt, ALU.mult)
                     for u in range(2):
-                        nc.tensor.transpose(da_bank[c][:, 2 * h + u, :], da[:].bitcast(F32)[:, u:PASS // 2:2], ident[:])
+                        nc.tensor.transpose(da_bank[c][:, 2 * h + u, :], da.bitcast(F32)[:, u:PASS // 2:2], ident[:])
             elif op == "do":
                 dt = keep.tile([P, H, PACK], BF16, name=f"da_turned{c}", align_bytes=64)
                 nc.scalar.copy(dt[:].rearrange("p i t -> p (i t)").bitcast(F32).rearrange("p (h i u) -> p h i u", h=2, u=2),
@@ -171,4 +180,4 @@ def tile_moe_mlp_relu_kernel(tc, xT, dyT, a, w2, gate, offs, out):
                         nc.sync.dma_start(out[1, h * P:(h + 1) * P, :], res[:])
                     else:
                         nc.scalar.copy(res[:], acc[h][:, 0:H])
-                        nc.sync.dma_start(out[1, h * P:(h + 1) * P, :], res[:])
+                        nc.scalar.dma_start(out[1, h * P:(h + 1) * P, :], res[:])

@@ -1,7 +1,6 @@
 from contextlib import ExitStack
 
 import concourse.mybir as mybir
-from concourse.masks import make_identity
 
 K, T, E, C, H, N = 256, 2560, 2, 1024, 256, 512
 FLOPS = 2 * E * C * (N * H + K * H)
@@ -20,10 +19,10 @@ PACK = 4
 PASS = P * PACK
 PASSES = E * C // PASS
 LIST_COLS = PASS // 16
-X_CUTS = [0,640,1280,1920,2560]
+X_CUTS = [0,768,1472,2176,2560]
 DY_CUT = 2304
-LOADS = "d0 d1 x0 x1 x2 x3 w0 w1 dA d3 dB A0 A1".split()
-STEPS = "D00 D01 D02 D03 D10 D11 D12 D13 P0 P1 P2 P3 W0 W1 X0 xo0 X1 xo1 X2 xo2 X3 xo3 Qw0 Qw1 D30 D20 I0 D31 D21 I1 D32 D22 I2 Qg0 D33 D23 I3 Qg1 S0 Qg2 S1 Qg3 S2 S3 do0 do1 do2 do3 Qd0 Qx0 m0 Qd1 Qx1 m1 Qd2 Qx2 m2 Qx3 Qd3 m3".split()
+LOADS = "d0 x0 d1 x1 x2 x3 w0 w1 dA d3 dB A0 A1".split()
+STEPS = "D00 D01 D02 D03 D10 D11 D12 D13 P0 P1 P2 P3 W0 W1 X0 xo0 X1 xo1 X2 xo2 X3 xo3 Qw0 Qw1 D30 D20 I0 D31 D21 I1 D32 D22 I2 Qg0 D33 D23 I3 Qg1 S0 Qg2 S1 Qg3 S2 S3 do0 do1 do2 dh0 dh1 Qd0 Qx0 Qd1 Qx1 m1 Qd2 Qx2 Qx3 Qh0 mh0 Qh1 mh1".split()
 
 
 def tile_moe_mlp_relu_kernel(tc, xT, dyT, a, w2, gate, offs, out):
@@ -39,7 +38,16 @@ def tile_moe_mlp_relu_kernel(tc, xT, dyT, a, w2, gate, offs, out):
         nc.sync.dma_start(offsets[:], offs)
 
         ident = keep.tile([P, P], F32, name="ident")
-        make_identity(nc, ident[:])
+        ones = keep.tile([P, 32], F32, name="ones")
+        count = keep.tile([P, 32], F32, name="count", align_bytes=64)
+        count_t = keep.tile([P, 32], F32, name="count_t", align_bytes=64)
+        nc.vector.memset(ones[:], 1.0)
+        nc.vector.memset(ident[:], 0.0)
+        nc.vector.tensor_tensor_scan(count[:], ones[:], ones[:], 0.0, ALU.mult, ALU.add)
+        nc.vector.transpose(count_t[:], count[:])
+        for q in range(4):
+            rows = slice(32 * q, 32 * q + 32)
+            nc.vector.tensor_tensor(ident[rows, rows], count[rows, :], count_t[rows, :], ALU.is_equal)
 
         dy_rows = dyT.rearrange("(p j) t -> j p t", j=PACK)
         dy = [keep.tile([P, T], F32, name=f"dy{j}") for j in range(PACK)]
@@ -144,18 +152,44 @@ def tile_moe_mlp_relu_kernel(tc, xT, dyT, a, w2, gate, offs, out):
                     nc.tensor.matmul_mx(dh[c, h][:], lhsT=wq[e][0][:, cols].bitcast(FP8X4), lhsT_scale=wq[e][1][:, cols],
                                         rhs=gq[c][0].bitcast(FP8X4), rhs_scale=gq[c][1][:], start=True, stop=True)
             elif op == "S":
-                da_bank[c] = turned_bank()
+                da_bank[c, 0] = turned_bank()
+                da_bank[c, 1] = turned_bank() if c == PASSES - 1 else da_bank[c, 0]
                 da_both = keep.tile([P, 2, PASS], BF16, name=f"da{c}", tag=f"g32_{(c + 1) % PASSES}")
                 for h in range(2):
                     da = da_both[:, h, :]
                     nc.vector.scalar_tensor_tensor(da, a_sb[e][:, h, (c % 2) * PASS:(c % 2 + 1) * PASS], 0.0, dh[c, h][:], ALU.is_gt, ALU.mult)
                     for u in range(2):
-                        nc.tensor.transpose(da_bank[c][:, 2 * h + u, :], da.bitcast(F32)[:, u:PASS // 2:2], ident[:])
+                        nc.tensor.transpose(da_bank[c, h][:, 2 * h + u, :], da.bitcast(F32)[:, u:PASS // 2:2], ident[:])
             elif op == "do":
                 dt = keep.tile([P, H, PACK], BF16, name=f"da_turned{c}", align_bytes=64)
                 nc.scalar.copy(dt[:].rearrange("p i t -> p (i t)").bitcast(F32).rearrange("p (h i u) -> p h i u", h=2, u=2),
-                               da_bank[c][:].rearrange("p (h u) i -> p h i u", u=2))
+                               da_bank[c, 0][:].rearrange("p (h u) i -> p h i u", u=2))
                 da_turned[c] = dt
+            elif op == "dh":
+                if c == 0:
+                    da_turned[3] = keep.tile([P, H, PACK], BF16, name="da_turned3", align_bytes=64)
+                    daq[3] = (keep.tile([P, H], U32, name="da3_codes", align_bytes=64)[:], keep.tile([P, H], U8, name="da3_scales", align_bytes=64))
+                nc.scalar.copy(da_turned[3][:, c * P:(c + 1) * P, :].rearrange("p i t -> p (i t)").bitcast(F32).rearrange("p (i u) -> p i u", u=2),
+                               da_bank[3, c][:, 2 * c:2 * c + 2, :].rearrange("p u i -> p i u"))
+            elif op == "Qh":
+                cols = slice(c * P, (c + 1) * P)
+                nc.vector.quantize_mx(out=daq[3][0][:, cols].bitcast(FP8X4), scales=daq[3][1][:, cols],
+                                      in_=da_turned[3][:, cols, :].rearrange("p w j -> p (w j)"))
+            elif op == "mh":
+                cols = slice(c * P, (c + 1) * P)
+                bank = psum.tile([P, PASS], F32, name=f"acc1_{c}", tag="dh", bufs=4)
+                for h in range(2):
+                    rows = slice(h * P, (h + 1) * P)
+                    for cc in (2, 3):
+                        nc.tensor.matmul_mx(bank[:, rows], lhsT=xq[cc][0][:, rows].bitcast(FP8X4), lhsT_scale=xq[cc][1][:, rows],
+                                            rhs=daq[cc][0][:, cols].bitcast(FP8X4), rhs_scale=daq[cc][1][:, cols], start=cc == 2, stop=cc == 3)
+                res = keep.tile([P, 2, P], F32, name=f"res1_{c}")
+                if c == 0:
+                    nc.scalar.copy(res[:].rearrange("p h i -> p (h i)"), bank[:, 0:2 * P])
+                    nc.scalar.dma_start(out[1].rearrange("(h p) i -> p h i", p=P)[:, :, cols], res[:])
+                else:
+                    nc.vector.tensor_copy(res[:].rearrange("p h i -> p (h i)"), bank[:, 0:2 * P])
+                    nc.sync.dma_start(out[1].rearrange("(h p) i -> p h i", p=P)[:, :, cols], res[:])
             elif op == "Qd":
                 daq[c] = quantize(da_turned[c], f"da{c}")
             elif c == 1:

@@ -13,16 +13,14 @@ U16 = mybir.dt.uint16
 U8 = mybir.dt.uint8
 FP8X4 = mybir.dt.float8_e4m3fn_x4
 ALU = mybir.AluOpType
+COPY = mybir.ActivationFunctionType.Copy
 
 P = 128
 PACK = 4
 PASS = P * PACK
 PASSES = E * C // PASS
 LIST_COLS = PASS // 16
-X_CUTS = [0,768,1472,2176,2560]
-DY_CUT = 2304
-LOADS = "d0 x0 d1 x1 x2 x3 w0 w1 dA d3 dB A0 A1".split()
-STEPS = "D00 D01 D02 D03 D10 D11 D12 D13 P0 P1 P2 P3 W0 W1 X0 xo0 X1 xo1 X2 xo2 X3 xo3 Qw0 Qw1 D30 D20 I0 D31 D21 I1 D32 D22 I2 Qg0 D33 D23 I3 Qg1 S0 Qg2 S1 Qg3 S2 S3 do0 do1 do2 dh0 dh1 Qd0 Qx0 Qd1 Qx1 m1 Qd2 Qx2 Qx3 Qh0 mh0 Qh1 mh1".split()
+HALF_T = T // 2
 
 
 def tile_moe_mlp_relu_kernel(tc, xT, dyT, a, w2, gate, offs, out):
@@ -51,167 +49,171 @@ def tile_moe_mlp_relu_kernel(tc, xT, dyT, a, w2, gate, offs, out):
 
         dy_rows = dyT.rearrange("(p j) t -> j p t", j=PACK)
         dy = [keep.tile([P, T], F32, name=f"dy{j}") for j in range(PACK)]
-        x_rows = xT.rearrange("(p e) t -> p e t", e=2)
-        x_raw = [keep.tile([P, 2, X_CUTS[q + 1] - X_CUTS[q]], F32, name=f"x_raw{q}") for q in range(len(X_CUTS) - 1)]
+        x_raw = [[keep.tile([P, HALF_T], F32, name=f"x_raw{h}_{s}", tag=f"x_raw{h}_{s}", align_bytes=64) for s in range(2)] for h in range(2)]
         w_raw = [keep.tile([P, PACK, H], F32, name=f"w_raw{e}") for e in range(E)]
         a_rows = a.rearrange("(h p) s -> p h s", p=P)
-        a_sb = [keep.tile([P, 2, C], F32, name=f"a_sb{e}", tag=f"a_sb{e}", align_bytes=64) for e in range(E)]
+        a_sb = [keep.tile([P, 2, C], F32, name=f"a_sb{e}") for e in range(E)]
 
-        for name in LOADS:
-            n = int(name[1:], 16)
-            if name == "dA":
-                nc.sync.dma_start(dy[2][:, :DY_CUT], dy_rows[2][:, :DY_CUT])
-            elif name == "dB":
-                nc.sync.dma_start(dy[2][:, DY_CUT:], dy_rows[2][:, DY_CUT:])
-            elif name[0] == "d":
-                nc.sync.dma_start(dy[n][:], dy_rows[n])
-            elif name[0] == "x":
-                nc.sync.dma_start(x_raw[n][:], x_rows[:, :, X_CUTS[n]:X_CUTS[n + 1]])
-            elif name[0] == "w":
-                nc.sync.dma_start(w_raw[n][:], w2[n].rearrange("(p j) i -> p j i", j=PACK))
-            else:
-                nc.sync.dma_start(a_sb[n][:], a_rows[:, :, n * C:(n + 1) * C])
+        def load_x(h):
+            for s in range(2):
+                nc.sync.dma_start(x_raw[h][s][:], xT[h * P:(h + 1) * P, s * HALF_T:(s + 1) * HALF_T])
 
-        def quantize(src, name, codes=None):
-            width = src.shape[1]
-            if codes is None:
-                codes = keep.tile([P, width], U32, name=name + "_codes", align_bytes=64)[:]
+        for j in range(PACK):
+            nc.sync.dma_start(dy[j][:], dy_rows[j])
+            if j % 2 == 0:
+                load_x(j // 2)
+        for e in range(E):
+            nc.sync.dma_start(w_raw[e][:], w2[e].rearrange("(p j) i -> p j i", j=PACK))
+            nc.sync.dma_start(a_sb[e][:], a_rows[:, :, e * C:(e + 1) * C])
+
+        def quantize(src, name, tag=None):
+            width = src.shape[1] // PACK
+            codes = keep.tile([P, width], U32, name=name + "_codes", tag=tag or name + "_codes", align_bytes=64)
             scales = keep.tile([P, width], U8, name=name + "_scales", align_bytes=64)
-            nc.vector.quantize_mx(out=codes.bitcast(FP8X4), scales=scales[:], in_=src[:].rearrange("p w j -> p (w j)"))
+            nc.vector.quantize_mx(out=codes[:].bitcast(FP8X4), scales=scales[:], in_=src)
             return codes, scales
+
+        def mx(dst, lhs, lhs_cols, rhs, rhs_cols, start, stop):
+            nc.tensor.matmul_mx(dst, lhsT=lhs[0][:, lhs_cols].bitcast(FP8X4), lhsT_scale=lhs[1][:, lhs_cols],
+                                rhs=rhs[0][:, rhs_cols].bitcast(FP8X4), rhs_scale=rhs[1][:, rhs_cols], start=start, stop=stop)
 
         def turned_bank():
             return psum.tile([P, PACK, P], F32, name="turned", tag="turned", bufs=4)
 
-        gate_sb = [keep.tile([P, PASS], F32, name=f"gate_sb{c}") for c in range(PASSES)]
+        def sum_bank():
+            return psum.tile([P, PASS], F32, name="sums", tag="sums", bufs=4)
+
+        gate_sb = [keep.tile([P, PASS], F32, name=f"gate_sb{c}", tag=f"gate_sb{c}", align_bytes=64) for c in range(PASSES)]
         for c in range(PASSES):
             bank = turned_bank()
             for i in range(PACK):
                 nc.tensor.transpose(bank[:, i, :], gate_cols[:, c, i:i + 1].to_broadcast([P, P]), ident[:])
             nc.scalar.copy(gate_sb[c][:].rearrange("q (p i) -> q p i", i=PACK), bank[:].rearrange("q i p -> q p i"))
 
-        g32 = [keep.tile([P, PACK, PASS], F32, name=f"g32_{c}", tag=f"g32_{c}") for c in range(PASSES)]
+        g32 = [keep.tile([P, PACK, PASS], F32, name=f"g32_{c}", tag=f"g32_{c}", align_bytes=64) for c in range(PASSES)]
 
-        def g_part(c, n):
-            return g32[c][:]
+        def gather_dy(j):
+            for c in range(PASSES):
+                nc.vector.tensor_tensor(g32[c][:, j, :], dy[j][:].indirect(offsets[:, c * LIST_COLS:(c + 1) * LIST_COLS]),
+                                        gate_sb[c][:], ALU.mult)
 
-        def gather_dy(j, c, n):
-            nc.vector.tensor_tensor(g_part(c, n)[:, j, :], dy[j][:].indirect(offsets[:, c * LIST_COLS:(c + n) * LIST_COLS]),
-                                    gate_sb[c][:], ALU.mult)
+        def interleave(copy, dst, src, run):
+            copy(dst.rearrange("p (c i) j -> p c j i", i=run), src.rearrange("p j (c i) -> p c j i", i=run))
 
-        x_pairs = keep.tile([P, T], U32, name="x_pairs")
-        x_pairs_bf = x_pairs[:].bitcast(BF16).rearrange("p (t e) -> p t e", e=2)
+        def turn_pairs(dst, src):
+            for u in range(2):
+                nc.tensor.transpose(dst[:, u, :], src.bitcast(F32)[:, u:PASS // 2:2], ident[:])
 
-        def interleave(dst, src):
-            nc.scalar.copy(dst.rearrange("p (c i) j -> p c j i", i=2), src.rearrange("p j (c i) -> p c j i", i=2))
+        def copy_turned(dst, src):
+            nc.scalar.copy(dst.rearrange("p r t -> p (r t)").bitcast(F32).rearrange("p (b r u) -> p b r u", r=P, u=2),
+                           src.rearrange("p (b u) r -> p b r u", u=2))
 
-        w_bf, x_bank, x_bf, g_bf, gq, wq, xq, daq, dh, da_bank, da_turned, acc = {}, {}, {}, {}, {}, {}, {}, {}, {}, {}, {}, {}
+        x_turned = {}
 
-        def second(dst, c, h):
-            cols = slice(h * P, (h + 1) * P)
-            nc.tensor.matmul_mx(dst, lhsT=xq[c][0][:, cols].bitcast(FP8X4), lhsT_scale=xq[c][1][:, cols],
-                                rhs=daq[c][0].bitcast(FP8X4), rhs_scale=daq[c][1][:], start=c % 2 == 0, stop=c % 2 == 1)
+        x_bf = [keep.tile([P, T], BF16, name=f"x_bf{h}") for h in range(2)]
 
-        for step in STEPS:
-            op, c = step[:-1], int(step[-1])
-            e = c // 2
-            if op[0] == "D":
-                gather_dy(int(op[1]), c, 1)
-            elif op[0] == "E":
-                gather_dy(int(op[1]), c, 2)
-            elif op[0] == "F":
-                gather_dy(int(op[1]), c, 4)
-            elif op == "P":
-                nc.scalar.copy(x_pairs_bf[:, X_CUTS[c]:X_CUTS[c + 1], :], x_raw[c][:].rearrange("p e t -> p t e"))
-            elif op == "W":
-                w_bf[c] = keep.tile([P, H, PACK], BF16, name=f"w_bf{c}", align_bytes=64)
-                interleave(w_bf[c][:], w_raw[c][:])
-            elif op == "Qw":
-                wq[c] = quantize(w_bf[c], f"w{c}")
-            elif op == "X":
-                xg = keep.tile([P, PASS], U32, name=f"x_slots{c}")
-                nc.vector.tensor_copy(xg[:], x_pairs[:].indirect(offsets[:, c * LIST_COLS:(c + 1) * LIST_COLS]))
-                x_bank[c] = turned_bank()
-                for t in range(PACK):
-                    nc.tensor.transpose(x_bank[c][:, t, :], xg[:].bitcast(F32)[:, t:PASS:PACK], ident[:])
-            elif op == "xo":
-                x_bf[c] = keep.tile([P, K, PACK], BF16, name=f"x_bf{c}", align_bytes=64)
-                nc.scalar.copy(x_bf[c][:], x_bank[c][:].rearrange("p t k -> p (t k)").bitcast(BF16).rearrange("p (t k) -> p k t", t=PACK))
-            elif op == "Qx":
-                if c == 0:
-                    x_codes = keep.tile([P, PASSES, K], U32, name="x_codes", tag="a_sb1", align_bytes=64)
-                xq[c] = quantize(x_bf[c], f"x{c}", x_codes[:, c, :])
-            elif op == "I":
-                g_bf[c] = keep.tile([P, PASS, PACK], BF16, name=f"g_bf{c}", align_bytes=64)
-                interleave(g_bf[c][:], g_part(c, 1))
-            elif op == "Qg":
-                gq[c] = quantize(g_bf[c], f"g{c}")
-                for h in range(2):
-                    dh[c, h] = psum.tile([P, PASS], F32, name="dh", tag="dh", bufs=4)
-                    cols = slice(h * P, (h + 1) * P)
-                    nc.tensor.matmul_mx(dh[c, h][:], lhsT=wq[e][0][:, cols].bitcast(FP8X4), lhsT_scale=wq[e][1][:, cols],
-                                        rhs=gq[c][0].bitcast(FP8X4), rhs_scale=gq[c][1][:], start=True, stop=True)
-            elif op == "S":
-                da_bank[c, 0] = turned_bank()
-                da_bank[c, 1] = turned_bank() if c == PASSES - 1 else da_bank[c, 0]
-                da_both = keep.tile([P, 2, PASS], BF16, name=f"da{c}", tag=f"g32_{(c + 1) % PASSES}")
-                for h in range(2):
-                    da = da_both[:, h, :]
-                    nc.vector.scalar_tensor_tensor(da, a_sb[e][:, h, (c % 2) * PASS:(c % 2 + 1) * PASS], 0.0, dh[c, h][:], ALU.is_gt, ALU.mult)
-                    for u in range(2):
-                        nc.tensor.transpose(da_bank[c, h][:, 2 * h + u, :], da.bitcast(F32)[:, u:PASS // 2:2], ident[:])
-            elif op == "do":
-                dt = keep.tile([P, H, PACK], BF16, name=f"da_turned{c}", align_bytes=64)
-                nc.scalar.copy(dt[:].rearrange("p i t -> p (i t)").bitcast(F32).rearrange("p (h i u) -> p h i u", h=2, u=2),
-                               da_bank[c, 0][:].rearrange("p (h u) i -> p h i u", u=2))
-                da_turned[c] = dt
-            elif op == "dh":
-                if c == 0:
-                    da_turned[3] = keep.tile([P, H, PACK], BF16, name="da_turned3", align_bytes=64)
-                    daq[3] = (keep.tile([P, H], U32, name="da3_codes", align_bytes=64)[:], keep.tile([P, H], U8, name="da3_scales", align_bytes=64))
-                nc.scalar.copy(da_turned[3][:, c * P:(c + 1) * P, :].rearrange("p i t -> p (i t)").bitcast(F32).rearrange("p (i u) -> p i u", u=2),
-                               da_bank[3, c][:, 2 * c:2 * c + 2, :].rearrange("p u i -> p i u"))
-            elif op == "Qh":
-                cols = slice(c * P, (c + 1) * P)
-                nc.vector.quantize_mx(out=daq[3][0][:, cols].bitcast(FP8X4), scales=daq[3][1][:, cols],
-                                      in_=da_turned[3][:, cols, :].rearrange("p w j -> p (w j)"))
-            elif op == "mh":
-                cols = slice(c * P, (c + 1) * P)
-                bank = psum.tile([P, PASS], F32, name=f"acc1_{c}", tag="dh", bufs=4)
-                for h in range(2):
-                    rows = slice(h * P, (h + 1) * P)
-                    for cc in (2, 3):
-                        nc.tensor.matmul_mx(bank[:, rows], lhsT=xq[cc][0][:, rows].bitcast(FP8X4), lhsT_scale=xq[cc][1][:, rows],
-                                            rhs=daq[cc][0][:, cols].bitcast(FP8X4), rhs_scale=daq[cc][1][:, cols], start=cc == 2, stop=cc == 3)
-                res = keep.tile([P, 2, P], F32, name=f"res1_{c}")
-                if c == 0:
-                    nc.scalar.copy(res[:].rearrange("p h i -> p (h i)"), bank[:, 0:2 * P])
-                    nc.scalar.dma_start(out[1].rearrange("(h p) i -> p h i", p=P)[:, :, cols], res[:])
-                else:
-                    nc.vector.tensor_copy(res[:].rearrange("p h i -> p (h i)"), bank[:, 0:2 * P])
-                    nc.sync.dma_start(out[1].rearrange("(h p) i -> p h i", p=P)[:, :, cols], res[:])
-            elif op == "Qd":
-                daq[c] = quantize(da_turned[c], f"da{c}")
-            elif c == 1:
-                bank = psum.tile([P, PASS], F32, name="acc0", tag="dh", bufs=4)
+        def round_x(h):
+            for s in range(2):
+                nc.scalar.copy(x_bf[h][:, s * HALF_T:(s + 1) * HALF_T], x_raw[h][s][:])
+
+        def gather_x(h, e, xg):
+            nc.scalar.activation(xg, x_bf[h][:].indirect(offsets[:, 2 * e * LIST_COLS:2 * (e + 1) * LIST_COLS]), COPY)
+            bank = turned_bank()
+            for cc in range(2):
+                turn_pairs(bank[:, 2 * cc:2 * cc + 2, :], xg[:, cc * PASS:(cc + 1) * PASS])
+            return bank
+
+        def copy_x(h, e, dst):
+            x_turned[h, e] = dst
+            copy_turned(dst.rearrange("p (r t) -> p r t", t=PACK), x_bank[h, e][:])
+
+        for j in range(PACK):
+            gather_dy(j)
+        x_bank = {}
+        for h in range(2):
+            round_x(h)
+            for e in range(E):
+                xg = keep.tile([P, C], BF16, name=f"x_slots{h}_{e}")
+                x_bank[h, e] = gather_x(h, e, xg[:])
+        copy_x(0, 0, keep.tile([P, C], BF16, name="x_turned0_0", align_bytes=64)[:])
+        copy_x(0, 1, keep.tile([P, C], BF16, name="x_turned0_1", tag="x_raw1_0", align_bytes=64)[:])
+
+        g_bf = []
+        for c in range(PASSES):
+            g_bf.append(keep.tile([P, PASS, PACK], BF16, name=f"g_bf{c}", align_bytes=64))
+            interleave(nc.scalar.copy, g_bf[c][:], g32[c][:], 2)
+
+        after = [keep.tile([P, 3 * C], BF16, name=f"after{c}", tag=f"g32_{c}", align_bytes=64) for c in range(PASSES)]
+        for e in range(E):
+            copy_x(1, e, after[PASSES - 1][:, (1 + e) * C:(2 + e) * C])
+
+        wq, xq, daq, da_bank = {}, {}, {}, {}
+
+        def quantize_w(e):
+            w_bf = keep.tile([P, H, PACK], BF16, name=f"w_bf{e}", align_bytes=64)
+            interleave(nc.vector.tensor_copy, w_bf[:], w_raw[e][:], 4)
+            wq[e] = quantize(w_bf[:].rearrange("p w j -> p (w j)"), f"w{e}")
+
+        def first_product(c):
+            gq = quantize(g_bf[c][:].rearrange("p w j -> p (w j)"), f"g{c}")
+            banks = [sum_bank() for h in range(2)]
+            for h in range(2):
+                mx(banks[h][:], wq[c // 2], slice(h * P, (h + 1) * P), gq, slice(0, PASS), True, True)
+            return banks
+
+        def mask_and_turn(c, dh):
+            last = c == PASSES - 1
+            da_bank[c, 0] = turned_bank()
+            da_bank[c, 1] = turned_bank() if last else da_bank[c, 0]
+            da = after[(c + 1) % PASSES][:, 0:C].rearrange("p (h s) -> p h s", h=2)
+            for h in range(2):
+                nc.vector.scalar_tensor_tensor(da[:, h, :], a_sb[c // 2][:, h, (c % 2) * PASS:(c % 2 + 1) * PASS], 0.0, dh[h][:],
+                                               ALU.is_gt, ALU.mult)
+                turn_pairs(da_bank[c, h][:, 2 * h:2 * h + 2, :], da[:, h, :])
+
+        for e in range(E):
+            quantize_w(e)
+
+        def quantize_x(h, e):
+            xq[h, e] = quantize(x_turned[h, e], f"x{h}_{e}", tag=f"gate_sb{2 * e + h}")
+
+        dh = {0: first_product(0)}
+        for c in range(PASSES):
+            if c + 1 < PASSES:
+                dh[c + 1] = first_product(c + 1)
+            mask_and_turn(c, dh[c])
+        for h in range(2):
+            for e in range(E):
+                quantize_x(h, e)
+
+        for c in range(PASSES - 1):
+            turned = keep.tile([P, H, PACK], BF16, name=f"da_turned{c}", align_bytes=64)
+            copy_turned(turned[:], da_bank[c, 0][:])
+            daq[c] = quantize(turned[:].rearrange("p w j -> p (w j)"), f"da{c}")
+            if c == 1:
+                bank = sum_bank()
                 for h in range(2):
                     for cc in range(2):
-                        second(bank[:, h * H:(h + 1) * H], cc, h)
+                        mx(bank[:, h * H:(h + 1) * H], xq[h, 0], slice(cc * P, (cc + 1) * P), daq[cc], slice(0, H), cc == 0, cc == 1)
                 res = keep.tile([P, 2, H], F32, name="res0")
-                nc.scalar.copy(res[:].rearrange("p h i -> p (h i)"), bank[:])
+                nc.vector.tensor_copy(res[:].rearrange("p h i -> p (h i)"), bank[:])
                 nc.sync.dma_start(out[0].rearrange("(h p) i -> p h i", p=P), res[:])
-            elif c == 2:
-                for h in range(2):
-                    acc[h] = psum.tile([P, PASS], F32, name=f"acc1_{h}", tag="dh", bufs=4)
-                    second(acc[h][:, 0:H], c, h)
-            elif c == 3:
-                for h in range(2):
-                    second(acc[h][:, 0:H], c, h)
-                for h in range(2):
-                    res = keep.tile([P, H], F32, name=f"res1_{h}")
-                    if h == 1:
-                        nc.vector.tensor_copy(res[:], acc[h][:, 0:H])
-                        nc.sync.dma_start(out[1, h * P:(h + 1) * P, :], res[:])
-                    else:
-                        nc.scalar.copy(res[:], acc[h][:, 0:H])
-                        nc.scalar.dma_start(out[1, h * P:(h + 1) * P, :], res[:])
+
+        last = PASSES - 1
+        for ih in range(2):
+            cols = slice(ih * P, (ih + 1) * P)
+            turned = keep.tile([P, P, PACK], BF16, name=f"da_turned{last}_{ih}", align_bytes=64)
+            copy_turned(turned[:], da_bank[last, ih][:, 2 * ih:2 * ih + 2, :])
+            half = quantize(turned[:].rearrange("p w j -> p (w j)"), f"da{last}_{ih}")
+            bank = sum_bank()
+            for h in range(2):
+                rows = slice(h * P, (h + 1) * P)
+                mx(bank[:, rows], xq[h, 1], slice(0, P), daq[last - 1], cols, True, False)
+                mx(bank[:, rows], xq[h, 1], slice(P, 2 * P), half, slice(0, P), False, True)
+            res = keep.tile([P, 2, P], F32, name=f"res1_{ih}")
+            if ih == 0:
+                nc.scalar.copy(res[:].rearrange("p h i -> p (h i)"), bank[:, 0:2 * P])
+                nc.scalar.dma_start(out[1].rearrange("(h p) i -> p h i", p=P)[:, :, cols], res[:])
+            else:
+                nc.vector.tensor_copy(res[:].rearrange("p h i -> p (h i)"), bank[:, 0:2 * P])
+                nc.sync.dma_start(out[1].rearrange("(h p) i -> p h i", p=P)[:, :, cols], res[:])

@@ -20,7 +20,7 @@ PACK = 4
 PASS = P * PACK
 PASSES = E * C // PASS
 LIST_COLS = PASS // 16
-HALF_T = T // 2
+X_CUTS = ((0, 896, 2048, T), (0, T // 2, T))
 
 
 def tile_moe_mlp_relu_kernel(tc, xT, dyT, a, w2, gate, offs, out):
@@ -49,33 +49,41 @@ def tile_moe_mlp_relu_kernel(tc, xT, dyT, a, w2, gate, offs, out):
 
         dy_rows = dyT.rearrange("(p j) t -> j p t", j=PACK)
         dy = [keep.tile([P, T], F32, name=f"dy{j}") for j in range(PACK)]
-        x_raw = [[keep.tile([P, HALF_T], F32, name=f"x_raw{h}_{s}", tag=f"x_raw{h}_{s}", align_bytes=64) for s in range(2)] for h in range(2)]
+        x_tags = (("x_raw0_0", "g32_1", "x_raw0_2"), ("x_raw1_0", "x_raw1_1"))
+        x_raw = [[keep.tile([P, X_CUTS[h][s + 1] - X_CUTS[h][s]], F32, name=f"x_raw{h}_{s}", tag=x_tags[h][s], align_bytes=64)
+                  for s in range(len(x_tags[h]))] for h in range(2)]
         w_raw = [keep.tile([P, PACK, H], F32, name=f"w_raw{e}") for e in range(E)]
         a_rows = a.rearrange("(h p) s -> p h s", p=P)
         a_sb = [keep.tile([P, 2, C], F32, name=f"a_sb{e}") for e in range(E)]
 
-        def load_x(h):
-            for s in range(2):
-                nc.sync.dma_start(x_raw[h][s][:], xT[h * P:(h + 1) * P, s * HALF_T:(s + 1) * HALF_T])
+        def load_x(h, s):
+            nc.sync.dma_start(x_raw[h][s][:], xT[h * P:(h + 1) * P, X_CUTS[h][s]:X_CUTS[h][s + 1]])
 
-        for j in range(PACK):
+        nc.sync.dma_start(dy[0][:], dy_rows[0])
+        for s in range(3):
+            load_x(0, s)
+        for j in range(1, PACK):
             nc.sync.dma_start(dy[j][:], dy_rows[j])
-            if j % 2 == 0:
-                load_x(j // 2)
+            if j < PACK - 1:
+                load_x(1, j - 1)
         for e in range(E):
             nc.sync.dma_start(w_raw[e][:], w2[e].rearrange("(p j) i -> p j i", j=PACK))
             nc.sync.dma_start(a_sb[e][:], a_rows[:, :, e * C:(e + 1) * C])
 
-        def quantize(src, name, tag=None):
+        def quantize(src, name, codes=None):
             width = src.shape[1] // PACK
-            codes = keep.tile([P, width], U32, name=name + "_codes", tag=tag or name + "_codes", align_bytes=64)
+            if codes is None:
+                codes = keep.tile([P, width], U32, name=name + "_codes", align_bytes=64)[:]
             scales = keep.tile([P, width], U8, name=name + "_scales", align_bytes=64)
-            nc.vector.quantize_mx(out=codes[:].bitcast(FP8X4), scales=scales[:], in_=src)
+            nc.vector.quantize_mx(out=codes.bitcast(FP8X4), scales=scales[:], in_=src)
             return codes, scales
 
         def mx(dst, lhs, lhs_cols, rhs, rhs_cols, start, stop):
             nc.tensor.matmul_mx(dst, lhsT=lhs[0][:, lhs_cols].bitcast(FP8X4), lhsT_scale=lhs[1][:, lhs_cols],
                                 rhs=rhs[0][:, rhs_cols].bitcast(FP8X4), rhs_scale=rhs[1][:, rhs_cols], start=start, stop=stop)
+
+        def half(c):
+            return slice((c % 2) * PASS, (c % 2 + 1) * PASS)
 
         def turned_bank():
             return psum.tile([P, PACK, P], F32, name="turned", tag="turned", bufs=4)
@@ -83,19 +91,30 @@ def tile_moe_mlp_relu_kernel(tc, xT, dyT, a, w2, gate, offs, out):
         def sum_bank():
             return psum.tile([P, PASS], F32, name="sums", tag="sums", bufs=4)
 
-        gate_sb = [keep.tile([P, PASS], F32, name=f"gate_sb{c}", tag=f"gate_sb{c}", align_bytes=64) for c in range(PASSES)]
+        gate_sb = [keep.tile([P, C], F32, name=f"gate_sb{e}", tag=f"gate_sb{e}", align_bytes=64) for e in range(E)]
         for c in range(PASSES):
             bank = turned_bank()
             for i in range(PACK):
                 nc.tensor.transpose(bank[:, i, :], gate_cols[:, c, i:i + 1].to_broadcast([P, P]), ident[:])
-            nc.scalar.copy(gate_sb[c][:].rearrange("q (p i) -> q p i", i=PACK), bank[:].rearrange("q i p -> q p i"))
+            nc.scalar.copy(gate_sb[c // 2][:, half(c)].rearrange("q (p i) -> q p i", i=PACK), bank[:].rearrange("q i p -> q p i"))
 
-        g32 = [keep.tile([P, PACK, PASS], F32, name=f"g32_{c}", tag=f"g32_{c}", align_bytes=64) for c in range(PASSES)]
+        x_bf = [keep.tile([P, T], BF16, name=f"x_bf{h}") for h in range(2)]
+
+        def round_x(copy, h, s):
+            copy(x_bf[h][:, X_CUTS[h][s]:X_CUTS[h][s + 1]], x_raw[h][s][:])
+
+        round_x(nc.scalar.copy, 0, 0)
+        round_x(nc.vector.tensor_copy, 0, 1)
+        round_x(nc.scalar.copy, 0, 2)
+
+        g32 = [keep.tile([P, PACK, C], F32, name=f"g32_{e}", tag=f"g32_{e}", align_bytes=64) for e in range(E)]
 
         def gather_dy(j):
-            for c in range(PASSES):
-                nc.vector.tensor_tensor(g32[c][:, j, :], dy[j][:].indirect(offsets[:, c * LIST_COLS:(c + 1) * LIST_COLS]),
-                                        gate_sb[c][:], ALU.mult)
+            width = PASS if j == PACK - 1 else C
+            for s in range(0, E * C, width):
+                cols = slice(s % C, s % C + width)
+                nc.vector.tensor_tensor(g32[s // C][:, j, cols], dy[j][:].indirect(offsets[:, s // 16:(s + width) // 16]),
+                                        gate_sb[s // C][:, cols], ALU.mult)
 
         def interleave(copy, dst, src, run):
             copy(dst.rearrange("p (c i) j -> p c j i", i=run), src.rearrange("p j (c i) -> p c j i", i=run))
@@ -110,18 +129,12 @@ def tile_moe_mlp_relu_kernel(tc, xT, dyT, a, w2, gate, offs, out):
 
         x_turned = {}
 
-        x_bf = [keep.tile([P, T], BF16, name=f"x_bf{h}") for h in range(2)]
-
-        def round_x(h):
-            for s in range(2):
-                nc.scalar.copy(x_bf[h][:, s * HALF_T:(s + 1) * HALF_T], x_raw[h][s][:])
-
-        def gather_x(h, e, xg):
-            nc.scalar.activation(xg, x_bf[h][:].indirect(offsets[:, 2 * e * LIST_COLS:2 * (e + 1) * LIST_COLS]), COPY)
-            bank = turned_bank()
-            for cc in range(2):
-                turn_pairs(bank[:, 2 * cc:2 * cc + 2, :], xg[:, cc * PASS:(cc + 1) * PASS])
-            return bank
+        def gather_x(h, c, xg, bank):
+            n = xg.shape[1] // PASS
+            nc.scalar.activation(xg, x_bf[h][:].indirect(offsets[:, c * LIST_COLS:(c + n) * LIST_COLS]), COPY)
+            for cc in range(n):
+                u = 2 * ((c + cc) % 2)
+                turn_pairs(bank[:, u:u + 2, :], xg[:, cc * PASS:(cc + 1) * PASS])
 
         def copy_x(h, e, dst):
             x_turned[h, e] = dst
@@ -131,21 +144,24 @@ def tile_moe_mlp_relu_kernel(tc, xT, dyT, a, w2, gate, offs, out):
             gather_dy(j)
         x_bank = {}
         for h in range(2):
-            round_x(h)
+            if h == 1:
+                for s in range(2):
+                    round_x(nc.scalar.copy, 1, s)
             for e in range(E):
-                xg = keep.tile([P, C], BF16, name=f"x_slots{h}_{e}")
-                x_bank[h, e] = gather_x(h, e, xg[:])
+                xg = keep.tile([P, PASS if (h, e) == (1, 1) else C], BF16, name=f"x_slots{h}_{e}", tag=f"x_slots{h}_{e}", align_bytes=64)
+                x_bank[h, e] = turned_bank()
+                gather_x(h, 2 * e, xg[:], x_bank[h, e])
         copy_x(0, 0, keep.tile([P, C], BF16, name="x_turned0_0", align_bytes=64)[:])
         copy_x(0, 1, keep.tile([P, C], BF16, name="x_turned0_1", tag="x_raw1_0", align_bytes=64)[:])
+        copy_x(1, 0, keep.tile([P, C], BF16, name="x_turned1_0", align_bytes=64)[:])
 
         g_bf = []
         for c in range(PASSES):
-            g_bf.append(keep.tile([P, PASS, PACK], BF16, name=f"g_bf{c}", align_bytes=64))
-            interleave(nc.scalar.copy, g_bf[c][:], g32[c][:], 2)
+            g_bf.append(keep.tile([P, PASS, PACK], BF16, name=f"g_bf{c}", tag=f"g_bf{c}", align_bytes=64))
+            interleave(nc.scalar.copy, g_bf[c][:], g32[c // 2][:, :, half(c)], 2)
 
-        after = [keep.tile([P, 3 * C], BF16, name=f"after{c}", tag=f"g32_{c}", align_bytes=64) for c in range(PASSES)]
-        for e in range(E):
-            copy_x(1, e, after[PASSES - 1][:, (1 + e) * C:(2 + e) * C])
+        late = keep.tile([P, PASS], BF16, name="x_slots_late", tag="g32_1", align_bytes=64)
+        gather_x(1, PASSES - 1, late[:], x_bank[1, 1])
 
         wq, xq, daq, da_bank = {}, {}, {}, {}
 
@@ -165,55 +181,64 @@ def tile_moe_mlp_relu_kernel(tc, xT, dyT, a, w2, gate, offs, out):
             last = c == PASSES - 1
             da_bank[c, 0] = turned_bank()
             da_bank[c, 1] = turned_bank() if last else da_bank[c, 0]
-            da = after[(c + 1) % PASSES][:, 0:C].rearrange("p (h s) -> p h s", h=2)
+            da_row = keep.tile([P, C], BF16, name=f"da{c}", tag=f"g_bf{(c + 1) % PASSES}", align_bytes=64)
+            da = da_row[:].rearrange("p (h s) -> p h s", h=2)
             for h in range(2):
-                nc.vector.scalar_tensor_tensor(da[:, h, :], a_sb[c // 2][:, h, (c % 2) * PASS:(c % 2 + 1) * PASS], 0.0, dh[h][:],
+                nc.vector.scalar_tensor_tensor(da[:, h, :], a_sb[c // 2][:, h, half(c)], 0.0, dh[h][:],
                                                ALU.is_gt, ALU.mult)
                 turn_pairs(da_bank[c, h][:, 2 * h:2 * h + 2, :], da[:, h, :])
 
         for e in range(E):
             quantize_w(e)
 
+        x_codes = [keep.tile([P, PACK * P], U32, name=f"x_codes{e}", tag=f"gate_sb{e}", align_bytes=64) for e in range(E)]
+
         def quantize_x(h, e):
-            xq[h, e] = quantize(x_turned[h, e], f"x{h}_{e}", tag=f"gate_sb{2 * e + h}")
+            xq[h, e] = quantize(x_turned[h, e], f"x{h}_{e}", x_codes[e][:, h * 2 * P:(h + 1) * 2 * P])
 
         dh = {0: first_product(0)}
         for c in range(PASSES):
             if c + 1 < PASSES:
                 dh[c + 1] = first_product(c + 1)
             mask_and_turn(c, dh[c])
-        for h in range(2):
-            for e in range(E):
-                quantize_x(h, e)
+        for h, e in ((0, 0), (1, 0), (0, 1)):
+            quantize_x(h, e)
 
         for c in range(PASSES - 1):
             turned = keep.tile([P, H, PACK], BF16, name=f"da_turned{c}", align_bytes=64)
             copy_turned(turned[:], da_bank[c, 0][:])
             daq[c] = quantize(turned[:].rearrange("p w j -> p (w j)"), f"da{c}")
             if c == 1:
+                copy_x(1, 1, keep.tile([P, C], BF16, name="x_turned1_1", align_bytes=64)[:])
+                quantize_x(1, 1)
                 bank = sum_bank()
                 for h in range(2):
                     for cc in range(2):
                         mx(bank[:, h * H:(h + 1) * H], xq[h, 0], slice(cc * P, (cc + 1) * P), daq[cc], slice(0, H), cc == 0, cc == 1)
-                res = keep.tile([P, 2, H], F32, name="res0")
-                nc.vector.tensor_copy(res[:].rearrange("p h i -> p (h i)"), bank[:])
-                nc.sync.dma_start(out[0].rearrange("(h p) i -> p h i", p=P), res[:])
+                bank0 = bank
 
         last = PASSES - 1
+        acc = {}
         for ih in range(2):
             cols = slice(ih * P, (ih + 1) * P)
             turned = keep.tile([P, P, PACK], BF16, name=f"da_turned{last}_{ih}", align_bytes=64)
             copy_turned(turned[:], da_bank[last, ih][:, 2 * ih:2 * ih + 2, :])
-            half = quantize(turned[:].rearrange("p w j -> p (w j)"), f"da{last}_{ih}")
-            bank = sum_bank()
+            piece = quantize(turned[:].rearrange("p w j -> p (w j)"), f"da{last}_{ih}")
+            acc[ih] = sum_bank()
             for h in range(2):
                 rows = slice(h * P, (h + 1) * P)
-                mx(bank[:, rows], xq[h, 1], slice(0, P), daq[last - 1], cols, True, False)
-                mx(bank[:, rows], xq[h, 1], slice(P, 2 * P), half, slice(0, P), False, True)
+                mx(acc[ih][:, rows], xq[h, 1], slice(0, P), daq[last - 1], cols, True, False)
+                mx(acc[ih][:, rows], xq[h, 1], slice(P, 2 * P), piece, slice(0, P), False, True)
+
+        res = keep.tile([P, 2, H], F32, name="res0")
+        nc.scalar.copy(res[:].rearrange("p h i -> p (h i)"), bank0[:])
+        nc.sync.dma_start(out[0].rearrange("(h p) i -> p h i", p=P), res[:])
+        for ih in range(2):
+            cols = slice(ih * P, (ih + 1) * P)
             res = keep.tile([P, 2, P], F32, name=f"res1_{ih}")
             if ih == 0:
-                nc.scalar.copy(res[:].rearrange("p h i -> p (h i)"), bank[:, 0:2 * P])
-                nc.scalar.dma_start(out[1].rearrange("(h p) i -> p h i", p=P)[:, :, cols], res[:])
-            else:
-                nc.vector.tensor_copy(res[:].rearrange("p h i -> p (h i)"), bank[:, 0:2 * P])
+                nc.vector.tensor_copy(res[:].rearrange("p h i -> p (h i)"), acc[ih][:, 0:2 * P])
                 nc.sync.dma_start(out[1].rearrange("(h p) i -> p h i", p=P)[:, :, cols], res[:])
+            else:
+                nc.scalar.copy(res[:].rearrange("p h i -> p (h i)"), acc[ih][:, 0:2 * P])
+                nc.scalar.dma_start(out[1].rearrange("(h p) i -> p h i", p=P)[:, :, cols], res[:])

@@ -31,8 +31,12 @@ def tile_moe_mlp_relu_kernel(tc, xT, dyT, a, w2, gate, offs, out):
 
         offsets = keep.tile([P, E * C // 16], U16, name="offsets")
 
-        gate_cols = keep.tile([P, PASSES, 8], F32, name="gate_cols")
-        nc.sync.dma_start(gate_cols[:, :, 0:PACK], gate[0].rearrange("(c p i) -> p c i", c=PASSES, i=PACK))
+        gate_cols = [keep.tile([P, 2 * PACK], F32, name=f"gate_cols{e}") for e in range(E)]
+
+        def load_gate(e):
+            nc.sync.dma_start(gate_cols[e][:], gate[e, e * C:(e + 1) * C].rearrange("(p m) -> p m", p=P))
+
+        load_gate(0)
         nc.sync.dma_start(offsets[:], offs)
 
         ident = keep.tile([P, P], F32, name="ident")
@@ -60,6 +64,7 @@ def tile_moe_mlp_relu_kernel(tc, xT, dyT, a, w2, gate, offs, out):
             nc.sync.dma_start(x_raw[h][s][:], xT[h * P:(h + 1) * P, X_CUTS[h][s]:X_CUTS[h][s + 1]])
 
         nc.sync.dma_start(dy[0][:], dy_rows[0])
+        load_gate(1)
         for s in range(3):
             load_x(0, s)
         for j in range(1, PACK):
@@ -92,11 +97,13 @@ def tile_moe_mlp_relu_kernel(tc, xT, dyT, a, w2, gate, offs, out):
             return psum.tile([P, PASS], F32, name="sums", tag="sums", bufs=4)
 
         gate_sb = [keep.tile([P, C], F32, name=f"gate_sb{e}", tag=f"gate_sb{e}", align_bytes=64) for e in range(E)]
-        for c in range(PASSES):
-            bank = turned_bank()
-            for i in range(PACK):
-                nc.tensor.transpose(bank[:, i, :], gate_cols[:, c, i:i + 1].to_broadcast([P, P]), ident[:])
-            nc.scalar.copy(gate_sb[c // 2][:, half(c)].rearrange("q (p i) -> q p i", i=PACK), bank[:].rearrange("q i p -> q p i"))
+        for e in range(E):
+            for b in range(2):
+                bank = turned_bank()
+                for i in range(PACK):
+                    m = PACK * b + i
+                    nc.tensor.transpose(bank[:, i, :], gate_cols[e][:, m:m + 1].to_broadcast([P, P]), ident[:])
+                nc.scalar.copy(gate_sb[e][:].rearrange("q (p b i) -> q p b i", b=2, i=PACK)[:, :, b, :], bank[:].rearrange("q i p -> q p i"))
 
         x_bf = [keep.tile([P, T], BF16, name=f"x_bf{h}") for h in range(2)]
 

@@ -52,7 +52,7 @@ def tile_moe_mlp_relu_kernel(tc, xT, dyT, a, w2, gate, offs, out):
             nc.vector.tensor_tensor(ident[rows, rows], count[rows, :], count_t[rows, :], ALU.is_equal)
 
         dy_rows = dyT.rearrange("(p j) t -> j p t", j=PACK)
-        dy = [keep.tile([P, T], F32, name=f"dy{j}") for j in range(PACK)]
+        dy = [keep.tile([P, T], F32, name=f"dy{j}", tag=f"dy{j}", align_bytes=64) for j in range(PACK)]
         x_tags = (("x_raw0_0", "g32_1", "x_raw0_2"), ("x_raw1_0", "x_raw1_1"))
         x_raw = [[keep.tile([P, X_CUTS[h][s + 1] - X_CUTS[h][s]], F32, name=f"x_raw{h}_{s}", tag=x_tags[h][s], align_bytes=64)
                   for s in range(len(x_tags[h]))] for h in range(2)]
@@ -67,12 +67,16 @@ def tile_moe_mlp_relu_kernel(tc, xT, dyT, a, w2, gate, offs, out):
         load_gate(1)
         for s in range(3):
             load_x(0, s)
-        for j in range(1, PACK):
-            nc.sync.dma_start(dy[j][:], dy_rows[j])
-            if j < PACK - 1:
-                load_x(1, j - 1)
-        for e in range(E):
+        def load_w(e):
             nc.sync.dma_start(w_raw[e][:], w2[e].rearrange("(p j) i -> p j i", j=PACK))
+
+        for j in range(1, PACK - 1):
+            nc.sync.dma_start(dy[j][:], dy_rows[j])
+            load_x(1, j - 1)
+        load_w(0)
+        nc.sync.dma_start(dy[PACK - 1][:], dy_rows[PACK - 1])
+        load_w(1)
+        for e in range(E):
             nc.sync.dma_start(a_sb[e][:], a_rows[:, :, e * C:(e + 1) * C])
 
         def quantize(src, name, codes=None):
@@ -162,6 +166,9 @@ def tile_moe_mlp_relu_kernel(tc, xT, dyT, a, w2, gate, offs, out):
         copy_x(0, 1, keep.tile([P, C], BF16, name="x_turned0_1", tag="x_raw1_0", align_bytes=64)[:])
         copy_x(1, 0, keep.tile([P, C], BF16, name="x_turned1_0", align_bytes=64)[:])
 
+        w_bf = [keep.tile([P, H, PACK], BF16, name=f"w_bf{e}", align_bytes=64) for e in range(E)]
+        interleave(nc.scalar.copy, w_bf[0][:], w_raw[0][:], 2)
+
         g_bf = []
         for c in range(PASSES):
             g_bf.append(keep.tile([P, PASS, PACK], BF16, name=f"g_bf{c}", tag=f"g_bf{c}", align_bytes=64))
@@ -173,9 +180,8 @@ def tile_moe_mlp_relu_kernel(tc, xT, dyT, a, w2, gate, offs, out):
         wq, xq, daq, da_bank = {}, {}, {}, {}
 
         def quantize_w(e):
-            w_bf = keep.tile([P, H, PACK], BF16, name=f"w_bf{e}", align_bytes=64)
-            interleave(nc.vector.tensor_copy, w_bf[:], w_raw[e][:], 4)
-            wq[e] = quantize(w_bf[:].rearrange("p w j -> p (w j)"), f"w{e}")
+            codes = keep.tile([P, H], U32, name=f"w{e}_codes", tag=f"dy{PACK - 1 - e}", align_bytes=64)
+            wq[e] = quantize(w_bf[e][:].rearrange("p w j -> p (w j)"), f"w{e}", codes[:])
 
         def first_product(c):
             gq = quantize(g_bf[c][:].rearrange("p w j -> p (w j)"), f"g{c}")
@@ -195,6 +201,7 @@ def tile_moe_mlp_relu_kernel(tc, xT, dyT, a, w2, gate, offs, out):
                                                ALU.is_gt, ALU.mult)
                 turn_pairs(da_bank[c, h][:, 2 * h:2 * h + 2, :], da[:, h, :])
 
+        interleave(nc.vector.tensor_copy, w_bf[1][:], w_raw[1][:], 4)
         for e in range(E):
             quantize_w(e)
 

@@ -20,7 +20,7 @@ PACK = 4
 PASS = P * PACK
 PASSES = E * C // PASS
 LIST_COLS = PASS // 16
-X_CUTS = ((0, 896, 2048, T), (0, T // 2, T))
+X_CUTS = ((0, T // 4, T // 2, 3 * T // 4, T), (0, T // 2, T))
 
 
 def tile_moe_mlp_relu_kernel(tc, xT, dyT, a, w2, gate, offs, out):
@@ -31,12 +31,8 @@ def tile_moe_mlp_relu_kernel(tc, xT, dyT, a, w2, gate, offs, out):
 
         offsets = keep.tile([P, E * C // 16], U16, name="offsets")
 
-        gate_cols = [keep.tile([P, 2 * PACK], F32, name=f"gate_cols{e}") for e in range(E)]
-
-        def load_gate(e):
-            nc.sync.dma_start(gate_cols[e][:], gate[e, e * C:(e + 1) * C].rearrange("(p m) -> p m", p=P))
-
-        load_gate(0)
+        gate_cols = keep.tile([P, E, 2 * PACK], F32, name="gate_cols")
+        nc.sync.dma_start(gate_cols[:], gate[0, :].rearrange("(e p m) -> p e m", e=E, p=P))
         nc.sync.dma_start(offsets[:], offs)
 
         ident = keep.tile([P, P], F32, name="ident")
@@ -53,7 +49,7 @@ def tile_moe_mlp_relu_kernel(tc, xT, dyT, a, w2, gate, offs, out):
 
         dy_rows = dyT.rearrange("(p j) t -> j p t", j=PACK)
         dy = [keep.tile([P, T], F32, name=f"dy{j}", tag=f"dy{j}", align_bytes=64) for j in range(PACK)]
-        x_tags = (("x_raw0_0", "g32_1", "x_raw0_2"), ("x_raw1_0", "x_raw1_1"))
+        x_tags = (("x_raw0_0", "x_raw0_1", "x_raw0_2", "x_raw0_3"), ("x_raw1_0", "x_raw1_1"))
         x_raw = [[keep.tile([P, X_CUTS[h][s + 1] - X_CUTS[h][s]], F32, name=f"x_raw{h}_{s}", tag=x_tags[h][s], align_bytes=64)
                   for s in range(len(x_tags[h]))] for h in range(2)]
         w_raw = [keep.tile([P, PACK, H], F32, name=f"w_raw{e}") for e in range(E)]
@@ -64,8 +60,7 @@ def tile_moe_mlp_relu_kernel(tc, xT, dyT, a, w2, gate, offs, out):
             nc.sync.dma_start(x_raw[h][s][:], xT[h * P:(h + 1) * P, X_CUTS[h][s]:X_CUTS[h][s + 1]])
 
         nc.sync.dma_start(dy[0][:], dy_rows[0])
-        load_gate(1)
-        for s in range(3):
+        for s in range(4):
             load_x(0, s)
         def load_w(e):
             nc.sync.dma_start(w_raw[e][:], w2[e].rearrange("(p j) i -> p j i", j=PACK))
@@ -106,7 +101,7 @@ def tile_moe_mlp_relu_kernel(tc, xT, dyT, a, w2, gate, offs, out):
                 bank = turned_bank()
                 for i in range(PACK):
                     m = PACK * b + i
-                    nc.tensor.transpose(bank[:, i, :], gate_cols[e][:, m:m + 1].to_broadcast([P, P]), ident[:])
+                    nc.tensor.transpose(bank[:, i, :], gate_cols[:, e, m:m + 1].to_broadcast([P, P]), ident[:])
                 nc.scalar.copy(gate_sb[e][:].rearrange("q (p b i) -> q p b i", b=2, i=PACK)[:, :, b, :], bank[:].rearrange("q i p -> q p i"))
 
         x_bf = [keep.tile([P, T], BF16, name=f"x_bf{h}") for h in range(2)]
@@ -114,9 +109,8 @@ def tile_moe_mlp_relu_kernel(tc, xT, dyT, a, w2, gate, offs, out):
         def round_x(copy, h, s):
             copy(x_bf[h][:, X_CUTS[h][s]:X_CUTS[h][s + 1]], x_raw[h][s][:])
 
-        round_x(nc.scalar.copy, 0, 0)
-        round_x(nc.vector.tensor_copy, 0, 1)
-        round_x(nc.scalar.copy, 0, 2)
+        for s in range(4):
+            round_x(nc.scalar.copy, 0, s)
 
         g32 = [keep.tile([P, PACK, C], F32, name=f"g32_{e}", tag=f"g32_{e}", align_bytes=64) for e in range(E)]
 
@@ -173,6 +167,8 @@ def tile_moe_mlp_relu_kernel(tc, xT, dyT, a, w2, gate, offs, out):
         for c in range(PASSES):
             g_bf.append(keep.tile([P, PASS, PACK], BF16, name=f"g_bf{c}", tag=f"g_bf{c}", align_bytes=64))
             interleave(nc.scalar.copy, g_bf[c][:], g32[c // 2][:, :, half(c)], 2)
+            if c == 1:
+                interleave(nc.scalar.copy, w_bf[1][:], w_raw[1][:], 2)
 
         late = keep.tile([P, PASS], BF16, name="x_slots_late", tag="g32_1", align_bytes=64)
         gather_x(1, PASSES - 1, late[:], x_bank[1, 1])
@@ -201,7 +197,6 @@ def tile_moe_mlp_relu_kernel(tc, xT, dyT, a, w2, gate, offs, out):
                                                ALU.is_gt, ALU.mult)
                 turn_pairs(da_bank[c, h][:, 2 * h:2 * h + 2, :], da[:, h, :])
 
-        interleave(nc.vector.tensor_copy, w_bf[1][:], w_raw[1][:], 4)
         for e in range(E):
             quantize_w(e)
 

@@ -21,12 +21,18 @@ PASS = P * PACK
 PASSES = E * C // PASS
 LIST_COLS = PASS // 16
 X_CUTS = ((0, T // 4, T // 2, 3 * T // 4, T), (0, T // 2, T))
+X_BY_VECTOR = 256
+HEAD = 3 * PASS
+G_BYTES = PASS * PACK * 2
+G_BY_SCALAR = 384
 
 
 def tile_moe_mlp_relu_kernel(tc, xT, dyT, a, w2, gate, offs, out):
     nc = tc.nc
     with ExitStack() as ctx:
         keep = ctx.enter_context(tc.tile_pool(name="keep", bufs=1))
+        laid = ctx.enter_context(tc.tile_pool(name="laid", bufs=1))
+        rows = ctx.enter_context(tc.tile_pool(name="rows", bufs=1))
         psum = ctx.enter_context(tc.psum_pool(name="psum", bufs=1))
 
         offsets = keep.tile([P, E * C // 16], U16, name="offsets")
@@ -44,20 +50,20 @@ def tile_moe_mlp_relu_kernel(tc, xT, dyT, a, w2, gate, offs, out):
         nc.vector.tensor_tensor_scan(count[:], ones[:], ones[:], 0.0, ALU.mult, ALU.add)
         nc.vector.transpose(count_t[:], count[:])
         for q in range(4):
-            rows = slice(32 * q, 32 * q + 32)
-            nc.vector.tensor_tensor(ident[rows, rows], count[rows, :], count_t[rows, :], ALU.is_equal)
+            quad = slice(32 * q, 32 * q + 32)
+            nc.vector.tensor_tensor(ident[quad, quad], count[quad, :], count_t[quad, :], ALU.is_equal)
 
         dy_rows = dyT.rearrange("(p j) t -> j p t", j=PACK)
         dy = [keep.tile([P, T], F32, name=f"dy{j}", tag=f"dy{j}", align_bytes=64) for j in range(PACK)]
-        x_tags = (("x_raw0_0", "x_raw0_1", "x_raw0_2", "x_raw0_3"), ("x_raw1_0", "x_raw1_1"))
-        x_raw = [[keep.tile([P, X_CUTS[h][s + 1] - X_CUTS[h][s]], F32, name=f"x_raw{h}_{s}", tag=x_tags[h][s], align_bytes=64)
-                  for s in range(len(x_tags[h]))] for h in range(2)]
+        x_first = keep.tile([P, T], F32, name="x_first", tag="g32_last", align_bytes=64)
+        x_raw = [[x_first[:, X_CUTS[0][s]:X_CUTS[0][s + 1]] for s in range(4)],
+                 [keep.tile([P, T // 2], F32, name=f"x_raw1_{s}", tag=f"x_raw1_{s}", align_bytes=64)[:] for s in range(2)]]
         w_raw = [keep.tile([P, PACK, H], F32, name=f"w_raw{e}") for e in range(E)]
         a_rows = a.rearrange("(h p) s -> p h s", p=P)
         a_sb = [keep.tile([P, 2, C], F32, name=f"a_sb{e}") for e in range(E)]
 
         def load_x(h, s):
-            nc.sync.dma_start(x_raw[h][s][:], xT[h * P:(h + 1) * P, X_CUTS[h][s]:X_CUTS[h][s + 1]])
+            nc.sync.dma_start(x_raw[h][s], xT[h * P:(h + 1) * P, X_CUTS[h][s]:X_CUTS[h][s + 1]])
 
         nc.sync.dma_start(dy[0][:], dy_rows[0])
         for s in range(4):
@@ -95,31 +101,31 @@ def tile_moe_mlp_relu_kernel(tc, xT, dyT, a, w2, gate, offs, out):
         def sum_bank():
             return psum.tile([P, PASS], F32, name="sums", tag="sums", bufs=4)
 
-        gate_sb = [keep.tile([P, C], F32, name=f"gate_sb{e}", tag=f"gate_sb{e}", align_bytes=64) for e in range(E)]
+        gate_sb = laid.tile([P, E * C], F32, name="gate_sb", offset=0, align_bytes=64)
         for e in range(E):
             for b in range(2):
                 bank = turned_bank()
                 for i in range(PACK):
                     m = PACK * b + i
                     nc.tensor.transpose(bank[:, i, :], gate_cols[:, e, m:m + 1].to_broadcast([P, P]), ident[:])
-                nc.scalar.copy(gate_sb[e][:].rearrange("q (p b i) -> q p b i", b=2, i=PACK)[:, :, b, :], bank[:].rearrange("q i p -> q p i"))
+                nc.scalar.copy(gate_sb[:, e * C:(e + 1) * C].rearrange("q (p b i) -> q p b i", b=2, i=PACK)[:, :, b, :], bank[:].rearrange("q i p -> q p i"))
 
         x_bf = [keep.tile([P, T], BF16, name=f"x_bf{h}") for h in range(2)]
 
         def round_x(copy, h, s):
-            copy(x_bf[h][:, X_CUTS[h][s]:X_CUTS[h][s + 1]], x_raw[h][s][:])
+            copy(x_bf[h][:, X_CUTS[h][s]:X_CUTS[h][s + 1]], x_raw[h][s])
 
         for s in range(4):
             round_x(nc.scalar.copy, 0, s)
 
-        g32 = [keep.tile([P, PACK, C], F32, name=f"g32_{e}", tag=f"g32_{e}", align_bytes=64) for e in range(E)]
+        g32_head = keep.tile([P, PACK, HEAD], F32, name="g32_head", align_bytes=64)
+        g32_last = keep.tile([P, PACK, PASS], F32, name="g32_last", tag="g32_last", align_bytes=64)
 
-        def gather_dy(j):
-            width = PASS if j == PACK - 1 else C
-            for s in range(0, E * C, width):
-                cols = slice(s % C, s % C + width)
-                nc.vector.tensor_tensor(g32[s // C][:, j, cols], dy[j][:].indirect(offsets[:, s // 16:(s + width) // 16]),
-                                        gate_sb[s // C][:, cols], ALU.mult)
+        def g32(j, lo, hi):
+            return g32_head[:, j, lo:hi] if lo < HEAD else g32_last[:, j, lo - HEAD:hi - HEAD]
+
+        def gather_dy(j, lo, hi):
+            nc.vector.tensor_tensor(g32(j, lo, hi), dy[j][:].indirect(offsets[:, lo // 16:hi // 16]), gate_sb[:, lo:hi], ALU.mult)
 
         def interleave(copy, dst, src, run):
             copy(dst.rearrange("p (c i) j -> p c j i", i=run), src.rearrange("p j (c i) -> p c j i", i=run))
@@ -136,7 +142,8 @@ def tile_moe_mlp_relu_kernel(tc, xT, dyT, a, w2, gate, offs, out):
 
         def gather_x(h, c, xg, bank):
             n = xg.shape[1] // PASS
-            nc.scalar.activation(xg, x_bf[h][:].indirect(offsets[:, c * LIST_COLS:(c + n) * LIST_COLS]), COPY)
+            own = n * PASS - X_BY_VECTOR if (h, c) == (0, 2) else n * PASS
+            nc.scalar.activation(xg[:, :own], x_bf[h][:].indirect(offsets[:, c * LIST_COLS:c * LIST_COLS + own // 16]), COPY)
             for cc in range(n):
                 u = 2 * ((c + cc) % 2)
                 turn_pairs(bank[:, u:u + 2, :], xg[:, cc * PASS:(cc + 1) * PASS])
@@ -145,73 +152,96 @@ def tile_moe_mlp_relu_kernel(tc, xT, dyT, a, w2, gate, offs, out):
             x_turned[h, e] = dst
             copy_turned(dst.rearrange("p (r t) -> p r t", t=PACK), x_bank[h, e][:])
 
-        for j in range(PACK):
-            gather_dy(j)
+        x_slots = {(h, e): keep.tile([P, PASS if (h, e) == (1, 1) else C], BF16, name=f"x_slots{h}_{e}", align_bytes=64)
+                   for h in range(2) for e in range(E)}
+        gather_dy(0, 0, C)
+        gather_dy(0, C, HEAD)
+        nc.vector.tensor_copy(x_slots[0, 1][:, C - X_BY_VECTOR:], x_first[:].indirect(offsets[:, (E * C - X_BY_VECTOR) // 16:]))
+        gather_dy(0, HEAD, E * C)
+        for j in range(1, PACK - 1):
+            gather_dy(j, 0, HEAD)
+            gather_dy(j, HEAD, E * C)
+        gather_dy(PACK - 1, 0, PASS)
+        gather_dy(PACK - 1, PASS, HEAD)
+        gather_dy(PACK - 1, HEAD, E * C)
         x_bank = {}
         for h in range(2):
             if h == 1:
                 for s in range(2):
                     round_x(nc.scalar.copy, 1, s)
             for e in range(E):
-                xg = keep.tile([P, PASS if (h, e) == (1, 1) else C], BF16, name=f"x_slots{h}_{e}", tag=f"x_slots{h}_{e}", align_bytes=64)
+                xg = x_slots[h, e]
                 x_bank[h, e] = turned_bank()
                 gather_x(h, 2 * e, xg[:], x_bank[h, e])
-        copy_x(0, 0, keep.tile([P, C], BF16, name="x_turned0_0", align_bytes=64)[:])
+        x_turned0 = keep.tile([P, 2 * C], BF16, name="x_turned0", align_bytes=64)
+        copy_x(0, 0, x_turned0[:, :C])
         copy_x(0, 1, keep.tile([P, C], BF16, name="x_turned0_1", tag="x_raw1_0", align_bytes=64)[:])
-        copy_x(1, 0, keep.tile([P, C], BF16, name="x_turned1_0", align_bytes=64)[:])
+        copy_x(1, 0, x_turned0[:, C:])
 
-        w_bf = [keep.tile([P, H, PACK], BF16, name=f"w_bf{e}", align_bytes=64) for e in range(E)]
-        interleave(nc.scalar.copy, w_bf[0][:], w_raw[0][:], 2)
+        w_bf0 = keep.tile([P, H, PACK], BF16, name="w_bf0", align_bytes=64)
+        interleave(nc.scalar.copy, w_bf0[:], w_raw[0][:], 2)
 
         g_bf = []
         for c in range(PASSES):
-            g_bf.append(keep.tile([P, PASS, PACK], BF16, name=f"g_bf{c}", tag=f"g_bf{c}", align_bytes=64))
-            interleave(nc.scalar.copy, g_bf[c][:], g32[c // 2][:, :, half(c)], 2)
-            if c == 1:
-                interleave(nc.scalar.copy, w_bf[1][:], w_raw[1][:], 2)
+            g_bf.append(rows.tile([P, PASS, PACK], BF16, name=f"g_bf{c}", offset=c * G_BYTES, align_bytes=64))
+            width = G_BY_SCALAR if c == 2 else PASS
+            interleave(nc.scalar.copy, g_bf[c][:, :width], g32(slice(None), c * PASS, c * PASS + width), 2)
 
-        late = keep.tile([P, PASS], BF16, name="x_slots_late", tag="g32_1", align_bytes=64)
-        gather_x(1, PASSES - 1, late[:], x_bank[1, 1])
+        wq, xq, daq, da_bank, w_bf1 = {}, {}, {}, {}, {}
 
-        wq, xq, daq, da_bank = {}, {}, {}, {}
+        def interleave_w1(h):
+            w_bf1[h] = rows.tile([P, P, PACK], BF16, name=f"w_bf1_{h}", offset=(h + 1) * G_BYTES + G_BYTES // 2, align_bytes=64)
+            nc.gpsimd.tensor_scalar(w_bf1[h][:], w_raw[1][:, :, h * P:(h + 1) * P].rearrange("p j i -> p i j"), 1.0, 0.0, ALU.mult, ALU.add)
 
-        def quantize_w(e):
-            codes = keep.tile([P, H], U32, name=f"w{e}_codes", tag=f"dy{PACK - 1 - e}", align_bytes=64)
-            wq[e] = quantize(w_bf[e][:].rearrange("p w j -> p (w j)"), f"w{e}", codes[:])
+        def quantize_g(c):
+            return quantize(g_bf[c][:].rearrange("p w j -> p (w j)"), f"g{c}")
 
-        def first_product(c):
-            gq = quantize(g_bf[c][:].rearrange("p w j -> p (w j)"), f"g{c}")
+        def first_product(c, gq):
             banks = [sum_bank() for h in range(2)]
             for h in range(2):
-                mx(banks[h][:], wq[c // 2], slice(h * P, (h + 1) * P), gq, slice(0, PASS), True, True)
+                w_codes, cols = wq[c // 2, h]
+                mx(banks[h][:], w_codes, cols, gq, slice(0, PASS), True, True)
             return banks
 
         def mask_and_turn(c, dh):
             last = c == PASSES - 1
             da_bank[c, 0] = turned_bank()
             da_bank[c, 1] = turned_bank() if last else da_bank[c, 0]
-            da_row = keep.tile([P, C], BF16, name=f"da{c}", tag=f"g_bf{(c + 1) % PASSES}", align_bytes=64)
+            da_row = rows.tile([P, C], BF16, name=f"da{c}", offset=(c + 1) % PASSES * G_BYTES, align_bytes=64)
             da = da_row[:].rearrange("p (h s) -> p h s", h=2)
             for h in range(2):
                 nc.vector.scalar_tensor_tensor(da[:, h, :], a_sb[c // 2][:, h, half(c)], 0.0, dh[h][:],
                                                ALU.is_gt, ALU.mult)
                 turn_pairs(da_bank[c, h][:, 2 * h:2 * h + 2, :], da[:, h, :])
 
-        for e in range(E):
-            quantize_w(e)
+        w0_codes = keep.tile([P, H], U32, name="w0_codes", tag=f"dy{PACK - 1}", align_bytes=64)
+        w0_q = quantize(w_bf0[:].rearrange("p w j -> p (w j)"), "w0", w0_codes[:])
+        for h in range(2):
+            wq[0, h] = (w0_q, slice(h * P, (h + 1) * P))
 
-        x_codes = [keep.tile([P, PACK * P], U32, name=f"x_codes{e}", tag=f"gate_sb{e}", align_bytes=64) for e in range(E)]
+        x_codes = [laid.tile([P, PACK * P], U32, name=f"x_codes{e}", offset=e * 4 * C, align_bytes=64) for e in range(E)]
 
         def quantize_x(h, e):
             xq[h, e] = quantize(x_turned[h, e], f"x{h}_{e}", x_codes[e][:, h * 2 * P:(h + 1) * 2 * P])
 
-        dh = {0: first_product(0)}
-        for c in range(PASSES):
-            if c + 1 < PASSES:
-                dh[c + 1] = first_product(c + 1)
+        xq0 = quantize(x_turned0[:], "x0", x_codes[0][:])
+        quantize_x(0, 1)
+        dh = {0: first_product(0, quantize_g(0))}
+        interleave(nc.vector.tensor_copy, g_bf[2][:, G_BY_SCALAR:], g32(slice(None), 2 * PASS + G_BY_SCALAR, HEAD), 4)
+        late = keep.tile([P, PASS], BF16, name="x_slots_late", tag="g32_last", align_bytes=64)
+        gather_x(1, PASSES - 1, late[:], x_bank[1, 1])
+        dh[1] = first_product(1, quantize_g(1))
+        interleave_w1(0)
+        mask_and_turn(0, dh[0])
+        gq2 = quantize_g(2)
+        interleave_w1(1)
+        mask_and_turn(1, dh[1])
+        for h in range(2):
+            wq[1, h] = (quantize(w_bf1[h][:].rearrange("p w j -> p (w j)"), f"w1_{h}"), slice(0, P))
+        dh[2] = first_product(2, gq2)
+        dh[3] = first_product(3, quantize_g(3))
+        for c in range(2, PASSES):
             mask_and_turn(c, dh[c])
-        for h, e in ((0, 0), (1, 0), (0, 1)):
-            quantize_x(h, e)
 
         for c in range(PASSES - 1):
             turned = keep.tile([P, H, PACK], BF16, name=f"da_turned{c}", align_bytes=64)
@@ -223,7 +253,7 @@ def tile_moe_mlp_relu_kernel(tc, xT, dyT, a, w2, gate, offs, out):
                 bank = sum_bank()
                 for h in range(2):
                     for cc in range(2):
-                        mx(bank[:, h * H:(h + 1) * H], xq[h, 0], slice(cc * P, (cc + 1) * P), daq[cc], slice(0, H), cc == 0, cc == 1)
+                        mx(bank[:, h * H:(h + 1) * H], xq0, slice((2 * h + cc) * P, (2 * h + cc + 1) * P), daq[cc], slice(0, H), cc == 0, cc == 1)
                 bank0 = bank
 
         last = PASSES - 1
@@ -235,9 +265,9 @@ def tile_moe_mlp_relu_kernel(tc, xT, dyT, a, w2, gate, offs, out):
             piece = quantize(turned[:].rearrange("p w j -> p (w j)"), f"da{last}_{ih}")
             acc[ih] = sum_bank()
             for h in range(2):
-                rows = slice(h * P, (h + 1) * P)
-                mx(acc[ih][:, rows], xq[h, 1], slice(0, P), daq[last - 1], cols, True, False)
-                mx(acc[ih][:, rows], xq[h, 1], slice(P, 2 * P), piece, slice(0, P), False, True)
+                block = slice(h * P, (h + 1) * P)
+                mx(acc[ih][:, block], xq[h, 1], slice(0, P), daq[last - 1], cols, True, False)
+                mx(acc[ih][:, block], xq[h, 1], slice(P, 2 * P), piece, slice(0, P), False, True)
 
         res = keep.tile([P, 2, H], F32, name="res0")
         nc.scalar.copy(res[:].rearrange("p h i -> p (h i)"), bank0[:])

@@ -22,9 +22,9 @@ PASSES = E * C // PASS
 LIST_COLS = PASS // 16
 X_CUTS = ((0, T // 4, T // 2, 3 * T // 4, T), (0, T // 2, T))
 X_BY_VECTOR = 256
-HEAD = 3 * PASS
 G_BYTES = PASS * PACK * 2
-G_BY_SCALAR = 384
+G32_CUTS = (0, 2 * PASS, 3 * PASS, 4 * PASS)
+G32_AT = tuple(PASSES * G_BYTES + 4 * PACK * s for s in G32_CUTS)
 
 
 def tile_moe_mlp_relu_kernel(tc, xT, dyT, a, w2, gate, offs, out):
@@ -55,7 +55,7 @@ def tile_moe_mlp_relu_kernel(tc, xT, dyT, a, w2, gate, offs, out):
 
         dy_rows = dyT.rearrange("(p j) t -> j p t", j=PACK)
         dy = [keep.tile([P, T], F32, name=f"dy{j}", tag=f"dy{j}", align_bytes=64) for j in range(PACK)]
-        x_first = keep.tile([P, T], F32, name="x_first", tag="g32_last", align_bytes=64)
+        x_first = rows.tile([P, T], F32, name="x_first", offset=G32_AT[2], align_bytes=64)
         x_raw = [[x_first[:, X_CUTS[0][s]:X_CUTS[0][s + 1]] for s in range(4)],
                  [keep.tile([P, T // 2], F32, name=f"x_raw1_{s}", tag=f"x_raw1_{s}", align_bytes=64)[:] for s in range(2)]]
         w_raw = [keep.tile([P, PACK, H], F32, name=f"w_raw{e}") for e in range(E)]
@@ -101,14 +101,14 @@ def tile_moe_mlp_relu_kernel(tc, xT, dyT, a, w2, gate, offs, out):
         def sum_bank():
             return psum.tile([P, PASS], F32, name="sums", tag="sums", bufs=4)
 
-        gate_sb = laid.tile([P, E * C], F32, name="gate_sb", offset=0, align_bytes=64)
+        gate_sb = [laid.tile([P, C], F32, name=f"gate_sb{e}", offset=4 * e * C, align_bytes=64) for e in range(E)]
         for e in range(E):
             for b in range(2):
                 bank = turned_bank()
                 for i in range(PACK):
                     m = PACK * b + i
                     nc.tensor.transpose(bank[:, i, :], gate_cols[:, e, m:m + 1].to_broadcast([P, P]), ident[:])
-                nc.scalar.copy(gate_sb[:, e * C:(e + 1) * C].rearrange("q (p b i) -> q p b i", b=2, i=PACK)[:, :, b, :], bank[:].rearrange("q i p -> q p i"))
+                nc.scalar.copy(gate_sb[e][:].rearrange("q (p b i) -> q p b i", b=2, i=PACK)[:, :, b, :], bank[:].rearrange("q i p -> q p i"))
 
         x_bf = [keep.tile([P, T], BF16, name=f"x_bf{h}") for h in range(2)]
 
@@ -118,14 +118,15 @@ def tile_moe_mlp_relu_kernel(tc, xT, dyT, a, w2, gate, offs, out):
         for s in range(4):
             round_x(nc.scalar.copy, 0, s)
 
-        g32_head = keep.tile([P, PACK, HEAD], F32, name="g32_head", align_bytes=64)
-        g32_last = keep.tile([P, PACK, PASS], F32, name="g32_last", tag="g32_last", align_bytes=64)
+        g32_tiles = [rows.tile([P, PACK, G32_CUTS[n + 1] - G32_CUTS[n]], F32, name=f"g32_{n}", offset=G32_AT[n], align_bytes=64) for n in range(3)]
 
         def g32(j, lo, hi):
-            return g32_head[:, j, lo:hi] if lo < HEAD else g32_last[:, j, lo - HEAD:hi - HEAD]
+            n = max(lo // PASS - 1, 0)
+            return g32_tiles[n][:, j, lo - G32_CUTS[n]:hi - G32_CUTS[n]]
 
         def gather_dy(j, lo, hi):
-            nc.vector.tensor_tensor(g32(j, lo, hi), dy[j][:].indirect(offsets[:, lo // 16:hi // 16]), gate_sb[:, lo:hi], ALU.mult)
+            nc.vector.tensor_tensor(g32(j, lo, hi), dy[j][:].indirect(offsets[:, lo // 16:hi // 16]),
+                                    gate_sb[lo // C][:, lo % C:lo % C + hi - lo], ALU.mult)
 
         def interleave(copy, dst, src, run):
             copy(dst.rearrange("p (c i) j -> p c j i", i=run), src.rearrange("p j (c i) -> p c j i", i=run))
@@ -154,16 +155,13 @@ def tile_moe_mlp_relu_kernel(tc, xT, dyT, a, w2, gate, offs, out):
 
         x_slots = {(h, e): keep.tile([P, PASS if (h, e) == (1, 1) else C], BF16, name=f"x_slots{h}_{e}", align_bytes=64)
                    for h in range(2) for e in range(E)}
-        gather_dy(0, 0, C)
-        gather_dy(0, C, HEAD)
-        nc.vector.tensor_copy(x_slots[0, 1][:, C - X_BY_VECTOR:], x_first[:].indirect(offsets[:, (E * C - X_BY_VECTOR) // 16:]))
-        gather_dy(0, HEAD, E * C)
-        for j in range(1, PACK - 1):
-            gather_dy(j, 0, HEAD)
-            gather_dy(j, HEAD, E * C)
-        gather_dy(PACK - 1, 0, PASS)
-        gather_dy(PACK - 1, PASS, HEAD)
-        gather_dy(PACK - 1, HEAD, E * C)
+        for j in range(PACK - 1):
+            for n in range(3):
+                if (j, n) == (0, 2):
+                    nc.vector.tensor_copy(x_slots[0, 1][:, C - X_BY_VECTOR:], x_first[:].indirect(offsets[:, (E * C - X_BY_VECTOR) // 16:]))
+                gather_dy(j, G32_CUTS[n], G32_CUTS[n + 1])
+        for c in range(PASSES):
+            gather_dy(PACK - 1, c * PASS, (c + 1) * PASS)
         x_bank = {}
         for h in range(2):
             if h == 1:
@@ -173,10 +171,10 @@ def tile_moe_mlp_relu_kernel(tc, xT, dyT, a, w2, gate, offs, out):
                 xg = x_slots[h, e]
                 x_bank[h, e] = turned_bank()
                 gather_x(h, 2 * e, xg[:], x_bank[h, e])
-        x_turned0 = keep.tile([P, 2 * C], BF16, name="x_turned0", align_bytes=64)
+        x_turned0 = keep.tile([P, 2 * C], BF16, name="x_turned0", tag="x_raw1_0", align_bytes=64)
         copy_x(0, 0, x_turned0[:, :C])
-        copy_x(0, 1, keep.tile([P, C], BF16, name="x_turned0_1", tag="x_raw1_0", align_bytes=64)[:])
-        copy_x(1, 0, x_turned0[:, C:])
+        copy_x(0, 1, x_turned0[:, C:])
+        copy_x(1, 0, keep.tile([P, C], BF16, name="x_turned1_0", align_bytes=64)[:])
 
         w_bf0 = keep.tile([P, H, PACK], BF16, name="w_bf0", align_bytes=64)
         interleave(nc.scalar.copy, w_bf0[:], w_raw[0][:], 2)
@@ -184,10 +182,9 @@ def tile_moe_mlp_relu_kernel(tc, xT, dyT, a, w2, gate, offs, out):
         g_bf = []
         for c in range(PASSES):
             g_bf.append(rows.tile([P, PASS, PACK], BF16, name=f"g_bf{c}", offset=c * G_BYTES, align_bytes=64))
-            width = G_BY_SCALAR if c == 2 else PASS
-            interleave(nc.scalar.copy, g_bf[c][:, :width], g32(slice(None), c * PASS, c * PASS + width), 2)
+            interleave(nc.scalar.copy, g_bf[c][:], g32(slice(None), c * PASS, (c + 1) * PASS), 2)
 
-        wq, xq, daq, da_bank, w_bf1 = {}, {}, {}, {}, {}
+        wq, xq1, daq, da_bank, w_bf1 = {}, {}, {}, {}, {}
 
         def interleave_w1(h):
             w_bf1[h] = rows.tile([P, P, PACK], BF16, name=f"w_bf1_{h}", offset=(h + 1) * G_BYTES + G_BYTES // 2, align_bytes=64)
@@ -207,28 +204,30 @@ def tile_moe_mlp_relu_kernel(tc, xT, dyT, a, w2, gate, offs, out):
             last = c == PASSES - 1
             da_bank[c, 0] = turned_bank()
             da_bank[c, 1] = turned_bank() if last else da_bank[c, 0]
-            da_row = rows.tile([P, C], BF16, name=f"da{c}", offset=(c + 1) % PASSES * G_BYTES, align_bytes=64)
+            da_row = rows.tile([P, C], BF16, name=f"da{c}", offset=0 if last else G32_AT[c], align_bytes=64)
             da = da_row[:].rearrange("p (h s) -> p h s", h=2)
             for h in range(2):
                 nc.vector.scalar_tensor_tensor(da[:, h, :], a_sb[c // 2][:, h, half(c)], 0.0, dh[h][:],
                                                ALU.is_gt, ALU.mult)
                 turn_pairs(da_bank[c, h][:, 2 * h:2 * h + 2, :], da[:, h, :])
 
-        w0_codes = keep.tile([P, H], U32, name="w0_codes", tag=f"dy{PACK - 1}", align_bytes=64)
+        x0_codes = keep.tile([P, PASS], U32, name="x0_codes", tag=f"dy{PACK - 2}", align_bytes=64)
+        xq0 = quantize(x_turned0[:], "x0", x0_codes[:])
+        w0_codes = laid.tile([P, H], U32, name="w0_codes", offset=0, align_bytes=64)
         w0_q = quantize(w_bf0[:].rearrange("p w j -> p (w j)"), "w0", w0_codes[:])
         for h in range(2):
             wq[0, h] = (w0_q, slice(h * P, (h + 1) * P))
 
-        x_codes = [laid.tile([P, PACK * P], U32, name=f"x_codes{e}", offset=e * 4 * C, align_bytes=64) for e in range(E)]
+        def quantize_x1(e):
+            codes = laid.tile([P, 2 * P], U32, name=f"x1_codes{e}", offset=(e + 1) * 4 * H, align_bytes=64)
+            xq1[e] = quantize(x_turned[1, e], f"x1_{e}", codes[:])
 
-        def quantize_x(h, e):
-            xq[h, e] = quantize(x_turned[h, e], f"x{h}_{e}", x_codes[e][:, h * 2 * P:(h + 1) * 2 * P])
+        def x_block(h, c):
+            return (xq0, slice(c * P, (c + 1) * P)) if h == 0 else (xq1[c // 2], slice(c % 2 * P, (c % 2 + 1) * P))
 
-        xq0 = quantize(x_turned0[:], "x0", x_codes[0][:])
-        quantize_x(0, 1)
+        quantize_x1(0)
         dh = {0: first_product(0, quantize_g(0))}
-        interleave(nc.vector.tensor_copy, g_bf[2][:, G_BY_SCALAR:], g32(slice(None), 2 * PASS + G_BY_SCALAR, HEAD), 4)
-        late = keep.tile([P, PASS], BF16, name="x_slots_late", tag="g32_last", align_bytes=64)
+        late = rows.tile([P, PASS], BF16, name="x_slots_late", offset=G32_AT[2] + G_BYTES, align_bytes=64)
         gather_x(1, PASSES - 1, late[:], x_bank[1, 1])
         dh[1] = first_product(1, quantize_g(1))
         interleave_w1(0)
@@ -249,11 +248,11 @@ def tile_moe_mlp_relu_kernel(tc, xT, dyT, a, w2, gate, offs, out):
             daq[c] = quantize(turned[:].rearrange("p w j -> p (w j)"), f"da{c}")
             if c == 1:
                 copy_x(1, 1, keep.tile([P, C], BF16, name="x_turned1_1", align_bytes=64)[:])
-                quantize_x(1, 1)
+                quantize_x1(1)
                 bank = sum_bank()
                 for h in range(2):
                     for cc in range(2):
-                        mx(bank[:, h * H:(h + 1) * H], xq0, slice((2 * h + cc) * P, (2 * h + cc + 1) * P), daq[cc], slice(0, H), cc == 0, cc == 1)
+                        mx(bank[:, h * H:(h + 1) * H], *x_block(h, cc), daq[cc], slice(0, H), cc == 0, cc == 1)
                 bank0 = bank
 
         last = PASSES - 1
@@ -266,8 +265,8 @@ def tile_moe_mlp_relu_kernel(tc, xT, dyT, a, w2, gate, offs, out):
             acc[ih] = sum_bank()
             for h in range(2):
                 block = slice(h * P, (h + 1) * P)
-                mx(acc[ih][:, block], xq[h, 1], slice(0, P), daq[last - 1], cols, True, False)
-                mx(acc[ih][:, block], xq[h, 1], slice(P, 2 * P), piece, slice(0, P), False, True)
+                mx(acc[ih][:, block], *x_block(h, last - 1), daq[last - 1], cols, True, False)
+                mx(acc[ih][:, block], *x_block(h, last), piece, slice(0, P), False, True)
 
         res = keep.tile([P, 2, H], F32, name="res0")
         nc.scalar.copy(res[:].rearrange("p h i -> p (h i)"), bank0[:])

@@ -25,6 +25,7 @@ X_BY_VECTOR = 256
 G_BYTES = PASS * PACK * 2
 G32_CUTS = (0, 2 * PASS, 3 * PASS, 4 * PASS)
 G32_AT = tuple(PASSES * G_BYTES + 4 * PACK * s for s in G32_CUTS)
+DA_AT = (G32_AT[0], G32_AT[0] + G_BYTES, G32_AT[2], 0)
 
 
 def tile_moe_mlp_relu_kernel(tc, xT, dyT, a, w2, gate, offs, out):
@@ -55,7 +56,7 @@ def tile_moe_mlp_relu_kernel(tc, xT, dyT, a, w2, gate, offs, out):
 
         dy_rows = dyT.rearrange("(p j) t -> j p t", j=PACK)
         dy = [keep.tile([P, T], F32, name=f"dy{j}", tag=f"dy{j}", align_bytes=64) for j in range(PACK)]
-        x_first = rows.tile([P, T], F32, name="x_first", offset=G32_AT[2], align_bytes=64)
+        x_first = keep.tile([P, T], F32, name="x_first", align_bytes=64)
         x_raw = [[x_first[:, X_CUTS[0][s]:X_CUTS[0][s + 1]] for s in range(4)],
                  [keep.tile([P, T // 2], F32, name=f"x_raw1_{s}", tag=f"x_raw1_{s}", align_bytes=64)[:] for s in range(2)]]
         w_raw = [keep.tile([P, PACK, H], F32, name=f"w_raw{e}") for e in range(E)]
@@ -157,9 +158,9 @@ def tile_moe_mlp_relu_kernel(tc, xT, dyT, a, w2, gate, offs, out):
                    for h in range(2) for e in range(E)}
         for j in range(PACK - 1):
             for n in range(3):
-                if (j, n) == (0, 2):
-                    nc.vector.tensor_copy(x_slots[0, 1][:, C - X_BY_VECTOR:], x_first[:].indirect(offsets[:, (E * C - X_BY_VECTOR) // 16:]))
                 gather_dy(j, G32_CUTS[n], G32_CUTS[n + 1])
+            if j == 0:
+                nc.vector.tensor_copy(x_slots[0, 1][:, C - X_BY_VECTOR:], x_first[:].indirect(offsets[:, (E * C - X_BY_VECTOR) // 16:]))
         for c in range(PASSES):
             gather_dy(PACK - 1, c * PASS, (c + 1) * PASS)
         x_bank = {}
@@ -184,11 +185,7 @@ def tile_moe_mlp_relu_kernel(tc, xT, dyT, a, w2, gate, offs, out):
             g_bf.append(rows.tile([P, PASS, PACK], BF16, name=f"g_bf{c}", offset=c * G_BYTES, align_bytes=64))
             interleave(nc.scalar.copy, g_bf[c][:], g32(slice(None), c * PASS, (c + 1) * PASS), 2)
 
-        wq, xq1, daq, da_bank, w_bf1 = {}, {}, {}, {}, {}
-
-        def interleave_w1(h):
-            w_bf1[h] = rows.tile([P, P, PACK], BF16, name=f"w_bf1_{h}", offset=(h + 1) * G_BYTES + G_BYTES // 2, align_bytes=64)
-            nc.gpsimd.tensor_scalar(w_bf1[h][:], w_raw[1][:, :, h * P:(h + 1) * P].rearrange("p j i -> p i j"), 1.0, 0.0, ALU.mult, ALU.add)
+        wq, xq1, daq, da_bank = {}, {}, {}, {}
 
         def quantize_g(c):
             return quantize(g_bf[c][:].rearrange("p w j -> p (w j)"), f"g{c}")
@@ -196,15 +193,14 @@ def tile_moe_mlp_relu_kernel(tc, xT, dyT, a, w2, gate, offs, out):
         def first_product(c, gq):
             banks = [sum_bank() for h in range(2)]
             for h in range(2):
-                w_codes, cols = wq[c // 2, h]
-                mx(banks[h][:], w_codes, cols, gq, slice(0, PASS), True, True)
+                mx(banks[h][:], wq[c // 2], slice(h * P, (h + 1) * P), gq, slice(0, PASS), True, True)
             return banks
 
         def mask_and_turn(c, dh):
             last = c == PASSES - 1
             da_bank[c, 0] = turned_bank()
             da_bank[c, 1] = turned_bank() if last else da_bank[c, 0]
-            da_row = rows.tile([P, C], BF16, name=f"da{c}", offset=0 if last else G32_AT[c], align_bytes=64)
+            da_row = rows.tile([P, C], BF16, name=f"da{c}", offset=DA_AT[c], align_bytes=64)
             da = da_row[:].rearrange("p (h s) -> p h s", h=2)
             for h in range(2):
                 nc.vector.scalar_tensor_tensor(da[:, h, :], a_sb[c // 2][:, h, half(c)], 0.0, dh[h][:],
@@ -214,38 +210,38 @@ def tile_moe_mlp_relu_kernel(tc, xT, dyT, a, w2, gate, offs, out):
         x0_codes = keep.tile([P, PASS], U32, name="x0_codes", tag=f"dy{PACK - 2}", align_bytes=64)
         xq0 = quantize(x_turned0[:], "x0", x0_codes[:])
         w0_codes = laid.tile([P, H], U32, name="w0_codes", offset=0, align_bytes=64)
-        w0_q = quantize(w_bf0[:].rearrange("p w j -> p (w j)"), "w0", w0_codes[:])
-        for h in range(2):
-            wq[0, h] = (w0_q, slice(h * P, (h + 1) * P))
+        wq[0] = quantize(w_bf0[:].rearrange("p w j -> p (w j)"), "w0", w0_codes[:])
 
         def quantize_x1(e):
-            codes = laid.tile([P, 2 * P], U32, name=f"x1_codes{e}", offset=(e + 1) * 4 * H, align_bytes=64)
+            codes = rows.tile([P, 2 * P], U32, name=f"x1_codes{e}", offset=G32_AT[1] + e * G_BYTES, align_bytes=64)
             xq1[e] = quantize(x_turned[1, e], f"x1_{e}", codes[:])
 
         def x_block(h, c):
             return (xq0, slice(c * P, (c + 1) * P)) if h == 0 else (xq1[c // 2], slice(c % 2 * P, (c % 2 + 1) * P))
 
-        quantize_x1(0)
-        dh = {0: first_product(0, quantize_g(0))}
-        late = rows.tile([P, PASS], BF16, name="x_slots_late", offset=G32_AT[2] + G_BYTES, align_bytes=64)
-        gather_x(1, PASSES - 1, late[:], x_bank[1, 1])
-        dh[1] = first_product(1, quantize_g(1))
-        interleave_w1(0)
-        mask_and_turn(0, dh[0])
-        gq2 = quantize_g(2)
-        interleave_w1(1)
-        mask_and_turn(1, dh[1])
-        for h in range(2):
-            wq[1, h] = (quantize(w_bf1[h][:].rearrange("p w j -> p (w j)"), f"w1_{h}"), slice(0, P))
-        dh[2] = first_product(2, gq2)
-        dh[3] = first_product(3, quantize_g(3))
-        for c in range(2, PASSES):
-            mask_and_turn(c, dh[c])
-
-        for c in range(PASSES - 1):
+        def quantize_da(c):
             turned = keep.tile([P, H, PACK], BF16, name=f"da_turned{c}", align_bytes=64)
             copy_turned(turned[:], da_bank[c, 0][:])
             daq[c] = quantize(turned[:].rearrange("p w j -> p (w j)"), f"da{c}")
+
+        dh = {c: first_product(c, quantize_g(c)) for c in range(2)}
+        w_bf1 = rows.tile([P, H, PACK], BF16, name="w_bf1", offset=G_BYTES + G_BYTES // 2, align_bytes=64)
+        nc.gpsimd.tensor_scalar(w_bf1[:], w_raw[1][:].rearrange("p j i -> p i j"), 1.0, 0.0, ALU.mult, ALU.add)
+        for c in range(2):
+            mask_and_turn(c, dh[c])
+        gq2 = quantize_g(2)
+        wq[1] = quantize(w_bf1[:].rearrange("p w j -> p (w j)"), "w1")
+        dh[2] = first_product(2, gq2)
+        quantize_x1(0)
+        dh[3] = first_product(3, quantize_g(3))
+        quantize_da(0)
+        late = rows.tile([P, PASS], BF16, name="x_slots_late", offset=G32_AT[2] + G_BYTES, align_bytes=64)
+        gather_x(1, PASSES - 1, late[:], x_bank[1, 1])
+        for c in range(2, PASSES):
+            mask_and_turn(c, dh[c])
+
+        for c in range(1, PASSES - 1):
+            quantize_da(c)
             if c == 1:
                 copy_x(1, 1, keep.tile([P, C], BF16, name="x_turned1_1", align_bytes=64)[:])
                 quantize_x1(1)

@@ -20,19 +20,14 @@ PACK = 4
 PASS = P * PACK
 PASSES = E * C // PASS
 LIST_COLS = PASS // 16
-X_CUTS = ((0, T // 4, T // 2, 3 * T // 4, T), (0, T // 2, T))
-X_BY_VECTOR = 256
-G_BYTES = PASS * PACK * 2
-G32_CUTS = (0, 2 * PASS, 3 * PASS, 4 * PASS)
-G32_AT = tuple(PASSES * G_BYTES + 4 * PACK * s for s in G32_CUTS)
-DA_AT = (G32_AT[0], G32_AT[0] + G_BYTES, G32_AT[2], 0)
+X_BY_VECTOR = 512
+G32_BYTES = PACK * C * 4
 
 
 def tile_moe_mlp_relu_kernel(tc, xT, dyT, a, w2, gate, offs, out):
     nc = tc.nc
     with ExitStack() as ctx:
         keep = ctx.enter_context(tc.tile_pool(name="keep", bufs=1))
-        laid = ctx.enter_context(tc.tile_pool(name="laid", bufs=1))
         rows = ctx.enter_context(tc.tile_pool(name="rows", bufs=1))
         psum = ctx.enter_context(tc.psum_pool(name="psum", bufs=1))
 
@@ -55,38 +50,35 @@ def tile_moe_mlp_relu_kernel(tc, xT, dyT, a, w2, gate, offs, out):
             nc.vector.tensor_tensor(ident[quad, quad], count[quad, :], count_t[quad, :], ALU.is_equal)
 
         dy_rows = dyT.rearrange("(p j) t -> j p t", j=PACK)
-        dy = [keep.tile([P, T], F32, name=f"dy{j}", tag=f"dy{j}", align_bytes=64) for j in range(PACK)]
-        x_first = keep.tile([P, T], F32, name="x_first", align_bytes=64)
-        x_raw = [[x_first[:, X_CUTS[0][s]:X_CUTS[0][s + 1]] for s in range(4)],
-                 [keep.tile([P, T // 2], F32, name=f"x_raw1_{s}", tag=f"x_raw1_{s}", align_bytes=64)[:] for s in range(2)]]
+        dy = [keep.tile([P, T], F32, name=f"dy{j}", align_bytes=64) for j in range(PACK)]
+        x = [keep.tile([P, T], F32, name=f"x{h}", align_bytes=64) for h in range(2)]
         w_raw = [keep.tile([P, PACK, H], F32, name=f"w_raw{e}") for e in range(E)]
         a_rows = a.rearrange("(h p) s -> p h s", p=P)
         a_sb = [keep.tile([P, 2, C], F32, name=f"a_sb{e}") for e in range(E)]
 
-        def load_x(h, s):
-            nc.sync.dma_start(x_raw[h][s], xT[h * P:(h + 1) * P, X_CUTS[h][s]:X_CUTS[h][s + 1]])
+        def load_x(h):
+            nc.sync.dma_start(x[h][:], xT[h * P:(h + 1) * P, :])
 
-        nc.sync.dma_start(dy[0][:], dy_rows[0])
-        for s in range(4):
-            load_x(0, s)
         def load_w(e):
             nc.sync.dma_start(w_raw[e][:], w2[e].rearrange("(p j) i -> p j i", j=PACK))
 
-        for j in range(1, PACK - 1):
-            nc.sync.dma_start(dy[j][:], dy_rows[j])
-            load_x(1, j - 1)
-        load_w(0)
-        nc.sync.dma_start(dy[PACK - 1][:], dy_rows[PACK - 1])
-        load_w(1)
-        for e in range(E):
+        def load_a(e):
             nc.sync.dma_start(a_sb[e][:], a_rows[:, :, e * C:(e + 1) * C])
 
-        def quantize(src, name, codes=None):
+        for j in range(PACK):
+            nc.sync.dma_start(dy[j][:], dy_rows[j])
+        load_w(0)
+        load_x(0)
+        load_a(0)
+        load_x(1)
+        load_w(1)
+        load_a(1)
+
+        def quantize(src, name):
             width = src.shape[1] // PACK
-            if codes is None:
-                codes = keep.tile([P, width], U32, name=name + "_codes", align_bytes=64)[:]
+            codes = keep.tile([P, width], U32, name=name + "_codes", align_bytes=64)
             scales = keep.tile([P, width], U8, name=name + "_scales", align_bytes=64)
-            nc.vector.quantize_mx(out=codes.bitcast(FP8X4), scales=scales[:], in_=src)
+            nc.vector.quantize_mx(out=codes[:].bitcast(FP8X4), scales=scales[:], in_=src)
             return codes, scales
 
         def mx(dst, lhs, lhs_cols, rhs, rhs_cols, start, stop):
@@ -102,167 +94,144 @@ def tile_moe_mlp_relu_kernel(tc, xT, dyT, a, w2, gate, offs, out):
         def sum_bank():
             return psum.tile([P, PASS], F32, name="sums", tag="sums", bufs=4)
 
-        gate_sb = [laid.tile([P, C], F32, name=f"gate_sb{e}", offset=4 * e * C, align_bytes=64) for e in range(E)]
+        gate_sb = [keep.tile([P, C], F32, name=f"gate_sb{e}", align_bytes=64) for e in range(E)]
         for e in range(E):
+            copy = nc.vector.tensor_copy if e == 0 else nc.scalar.copy
             for b in range(2):
                 bank = turned_bank()
                 for i in range(PACK):
                     m = PACK * b + i
                     nc.tensor.transpose(bank[:, i, :], gate_cols[:, e, m:m + 1].to_broadcast([P, P]), ident[:])
-                nc.scalar.copy(gate_sb[e][:].rearrange("q (p b i) -> q p b i", b=2, i=PACK)[:, :, b, :], bank[:].rearrange("q i p -> q p i"))
+                copy(gate_sb[e][:].rearrange("q (p b i) -> q p b i", b=2, i=PACK)[:, :, b, :], bank[:].rearrange("q i p -> q p i"))
 
-        x_bf = [keep.tile([P, T], BF16, name=f"x_bf{h}") for h in range(2)]
+        def entries(lo, hi):
+            return offsets[:, lo // 16:hi // 16]
 
-        def round_x(copy, h, s):
-            copy(x_bf[h][:, X_CUTS[h][s]:X_CUTS[h][s + 1]], x_raw[h][s])
+        g32 = [rows.tile([P, PACK, C], F32, name=f"g32_{e}", offset=e * G32_BYTES, align_bytes=64) for e in range(E)]
+        for j in range(PACK):
+            nc.vector.tensor_tensor(g32[0][:, j, :], dy[j][:].indirect(entries(0, C)), gate_sb[0][:], ALU.mult)
+            nc.scalar.activation(g32[1][:, j, :], dy[j][:].indirect(entries(C, 2 * C)), COPY)
 
-        for s in range(4):
-            round_x(nc.scalar.copy, 0, s)
+        def woven(dst):
+            return dst.rearrange("p (c i) j -> p c j i", i=2)
 
-        g32_tiles = [rows.tile([P, PACK, G32_CUTS[n + 1] - G32_CUTS[n]], F32, name=f"g32_{n}", offset=G32_AT[n], align_bytes=64) for n in range(3)]
+        def planes(src):
+            return src.rearrange("p j (c i) -> p c j i", i=2)
 
-        def g32(j, lo, hi):
-            n = max(lo // PASS - 1, 0)
-            return g32_tiles[n][:, j, lo - G32_CUTS[n]:hi - G32_CUTS[n]]
-
-        def gather_dy(j, lo, hi):
-            nc.vector.tensor_tensor(g32(j, lo, hi), dy[j][:].indirect(offsets[:, lo // 16:hi // 16]),
-                                    gate_sb[lo // C][:, lo % C:lo % C + hi - lo], ALU.mult)
-
-        def interleave(copy, dst, src, run):
-            copy(dst.rearrange("p (c i) j -> p c j i", i=run), src.rearrange("p j (c i) -> p c j i", i=run))
+        def flat(tile):
+            return tile[:].rearrange("p w j -> p (w j)")
 
         def turn_pairs(dst, src):
             for u in range(2):
                 nc.tensor.transpose(dst[:, u, :], src.bitcast(F32)[:, u:PASS // 2:2], ident[:])
 
         def copy_turned(dst, src):
-            nc.scalar.copy(dst.rearrange("p r t -> p (r t)").bitcast(F32).rearrange("p (b r u) -> p b r u", r=P, u=2),
+            nc.scalar.copy(dst.bitcast(F32).rearrange("p (b r u) -> p b r u", r=P, u=2),
                            src.rearrange("p (b u) r -> p b r u", u=2))
 
-        x_turned = {}
-
-        def gather_x(h, c, xg, bank):
-            n = xg.shape[1] // PASS
-            own = n * PASS - X_BY_VECTOR if (h, c) == (0, 2) else n * PASS
-            nc.scalar.activation(xg[:, :own], x_bf[h][:].indirect(offsets[:, c * LIST_COLS:c * LIST_COLS + own // 16]), COPY)
-            for cc in range(n):
-                u = 2 * ((c + cc) % 2)
-                turn_pairs(bank[:, u:u + 2, :], xg[:, cc * PASS:(cc + 1) * PASS])
-
-        def copy_x(h, e, dst):
-            x_turned[h, e] = dst
-            copy_turned(dst.rearrange("p (r t) -> p r t", t=PACK), x_bank[h, e][:])
-
-        x_slots = {(h, e): keep.tile([P, PASS if (h, e) == (1, 1) else C], BF16, name=f"x_slots{h}_{e}", align_bytes=64)
-                   for h in range(2) for e in range(E)}
-        for j in range(PACK - 1):
-            for n in range(3):
-                gather_dy(j, G32_CUTS[n], G32_CUTS[n + 1])
-            if j == 0:
-                nc.vector.tensor_copy(x_slots[0, 1][:, C - X_BY_VECTOR:], x_first[:].indirect(offsets[:, (E * C - X_BY_VECTOR) // 16:]))
-        for c in range(PASSES):
-            gather_dy(PACK - 1, c * PASS, (c + 1) * PASS)
-        x_bank = {}
-        for h in range(2):
-            if h == 1:
-                for s in range(2):
-                    round_x(nc.scalar.copy, 1, s)
-            for e in range(E):
-                xg = x_slots[h, e]
-                x_bank[h, e] = turned_bank()
-                gather_x(h, 2 * e, xg[:], x_bank[h, e])
-        x_turned0 = keep.tile([P, 2 * C], BF16, name="x_turned0", tag="x_raw1_0", align_bytes=64)
-        copy_x(0, 0, x_turned0[:, :C])
-        copy_x(0, 1, x_turned0[:, C:])
-        copy_x(1, 0, keep.tile([P, C], BF16, name="x_turned1_0", align_bytes=64)[:])
-
         w_bf0 = keep.tile([P, H, PACK], BF16, name="w_bf0", align_bytes=64)
-        interleave(nc.scalar.copy, w_bf0[:], w_raw[0][:], 2)
+        nc.scalar.copy(woven(w_bf0[:]), planes(w_raw[0][:]))
 
-        g_bf = []
-        for c in range(PASSES):
-            g_bf.append(rows.tile([P, PASS, PACK], BF16, name=f"g_bf{c}", offset=c * G_BYTES, align_bytes=64))
-            interleave(nc.scalar.copy, g_bf[c][:], g32(slice(None), c * PASS, (c + 1) * PASS), 2)
+        g_bf = [keep.tile([P, C, PACK], BF16, name=f"g_bf{e}", align_bytes=64) for e in range(E)]
+        nc.vector.tensor_copy(woven(g_bf[0][:]), planes(g32[0][:]))
 
-        wq, xq1, daq, da_bank = {}, {}, {}, {}
+        def gate_and_weave(c):
+            gates = gate_sb[1][:, half(c)].rearrange("p (c i) -> p c i", i=2).unsqueeze(2).to_broadcast([P, PASS // 2, PACK, 2])
+            nc.vector.tensor_tensor(woven(g_bf[1][:, half(c), :]), planes(g32[1][:, :, half(c)]), gates, ALU.mult)
 
-        def quantize_g(c):
-            return quantize(g_bf[c][:].rearrange("p w j -> p (w j)"), f"g{c}")
+        x_slots = [keep.tile([P, E * C], BF16, name=f"x_slots{h}", align_bytes=64) for h in range(2)]
+        x_turned = [keep.tile([P, 2, C], BF16, name=f"x_turned{e}", align_bytes=64) for e in range(E)]
+        x_bank = {}
 
-        def first_product(c, gq):
+        def turn_x(h, lo, hi):
+            for c in range(lo // PASS, hi // PASS):
+                if c % 2 == 0:
+                    x_bank[h, c // 2] = turned_bank()
+                u = 2 * (c % 2)
+                turn_pairs(x_bank[h, c // 2][:, u:u + 2, :], x_slots[h][:, c * PASS:(c + 1) * PASS])
+
+        def gather_x(h, lo, hi):
+            nc.scalar.activation(x_slots[h][:, lo:hi], x[h][:].indirect(entries(lo, hi)), COPY)
+            turn_x(h, lo, hi)
+
+        def copy_x(h, e):
+            copy_turned(x_turned[e][:, h, :], x_bank[h, e][:])
+
+        def first_product(c, wq, gq):
             banks = [sum_bank() for h in range(2)]
             for h in range(2):
-                mx(banks[h][:], wq[c // 2], slice(h * P, (h + 1) * P), gq, slice(0, PASS), True, True)
+                mx(banks[h][:], wq, slice(h * P, (h + 1) * P), gq, half(c), True, True)
             return banks
+
+        da_bank = {}
 
         def mask_and_turn(c, dh):
             last = c == PASSES - 1
             da_bank[c, 0] = turned_bank()
             da_bank[c, 1] = turned_bank() if last else da_bank[c, 0]
-            da_row = rows.tile([P, C], BF16, name=f"da{c}", offset=DA_AT[c], align_bytes=64)
-            da = da_row[:].rearrange("p (h s) -> p h s", h=2)
+            da = keep.tile([P, 2, PASS], BF16, name=f"da{c}", align_bytes=64)
             for h in range(2):
                 nc.vector.scalar_tensor_tensor(da[:, h, :], a_sb[c // 2][:, h, half(c)], 0.0, dh[h][:],
                                                ALU.is_gt, ALU.mult)
                 turn_pairs(da_bank[c, h][:, 2 * h:2 * h + 2, :], da[:, h, :])
 
-        x0_codes = keep.tile([P, PASS], U32, name="x0_codes", tag=f"dy{PACK - 2}", align_bytes=64)
-        xq0 = quantize(x_turned0[:], "x0", x0_codes[:])
-        w0_codes = laid.tile([P, H], U32, name="w0_codes", offset=0, align_bytes=64)
-        wq[0] = quantize(w_bf0[:].rearrange("p w j -> p (w j)"), "w0", w0_codes[:])
-
-        def quantize_x1(e):
-            codes = rows.tile([P, 2 * P], U32, name=f"x1_codes{e}", offset=G32_AT[1] + e * G_BYTES, align_bytes=64)
-            xq1[e] = quantize(x_turned[1, e], f"x1_{e}", codes[:])
-
-        def x_block(h, c):
-            return (xq0, slice(c * P, (c + 1) * P)) if h == 0 else (xq1[c // 2], slice(c % 2 * P, (c % 2 + 1) * P))
-
-        def quantize_da(c):
-            turned = keep.tile([P, H, PACK], BF16, name=f"da_turned{c}", align_bytes=64)
-            copy_turned(turned[:], da_bank[c, 0][:])
-            daq[c] = quantize(turned[:].rearrange("p w j -> p (w j)"), f"da{c}")
-
-        dh = {c: first_product(c, quantize_g(c)) for c in range(2)}
-        w_bf1 = rows.tile([P, H, PACK], BF16, name="w_bf1", offset=G_BYTES + G_BYTES // 2, align_bytes=64)
+        gate_and_weave(2)
+        gq0 = quantize(flat(g_bf[0]), "g0")
+        wq0 = quantize(flat(w_bf0), "w0")
+        gather_x(0, 0, C)
+        gather_x(0, C, C + PASS)
+        gather_x(0, C + PASS, 2 * C)
+        dh = {c: first_product(c, wq0, gq0) for c in range(2)}
+        gate_and_weave(3)
+        copy_x(0, 0)
+        copy_x(0, 1)
+        w_bf1 = rows.tile([P, H, PACK], BF16, name="w_bf1", offset=G32_BYTES, align_bytes=64)
         nc.gpsimd.tensor_scalar(w_bf1[:], w_raw[1][:].rearrange("p j i -> p i j"), 1.0, 0.0, ALU.mult, ALU.add)
+        gather_x(1, 0, C)
         for c in range(2):
             mask_and_turn(c, dh[c])
-        gq2 = quantize_g(2)
-        wq[1] = quantize(w_bf1[:].rearrange("p w j -> p (w j)"), "w1")
-        dh[2] = first_product(2, gq2)
-        quantize_x1(0)
-        dh[3] = first_product(3, quantize_g(3))
-        quantize_da(0)
-        late = rows.tile([P, PASS], BF16, name="x_slots_late", offset=G32_AT[2] + G_BYTES, align_bytes=64)
-        gather_x(1, PASSES - 1, late[:], x_bank[1, 1])
+        gather_x(1, C, 2 * C - X_BY_VECTOR)
+        gq1 = quantize(flat(g_bf[1]), "g1")
+        wq1 = quantize(flat(w_bf1), "w1")
+        for c in range(2, PASSES):
+            dh[c] = first_product(c, wq1, gq1)
+        nc.vector.tensor_copy(x_slots[1][:, 2 * C - X_BY_VECTOR:], x[1][:].indirect(entries(2 * C - X_BY_VECTOR, 2 * C)))
+        turn_x(1, 2 * C - X_BY_VECTOR, 2 * C)
+        copy_x(1, 0)
+        da_turned0 = keep.tile([P, 2, C], BF16, name="da_turned0", align_bytes=64)
+        for c in range(2):
+            copy_turned(da_turned0[:, c, :], da_bank[c, 0][:])
+        copy_x(1, 1)
         for c in range(2, PASSES):
             mask_and_turn(c, dh[c])
 
-        for c in range(1, PASSES - 1):
-            quantize_da(c)
-            if c == 1:
-                copy_x(1, 1, keep.tile([P, C], BF16, name="x_turned1_1", align_bytes=64)[:])
-                quantize_x1(1)
-                bank = sum_bank()
-                for h in range(2):
-                    for cc in range(2):
-                        mx(bank[:, h * H:(h + 1) * H], *x_block(h, cc), daq[cc], slice(0, H), cc == 0, cc == 1)
-                bank0 = bank
+        def x_cols(h, cc):
+            return slice((2 * h + cc) * P, (2 * h + cc + 1) * P)
+
+        xq0 = quantize(x_turned[0][:].rearrange("p h w -> p (h w)"), "x0")
+        daq0 = quantize(da_turned0[:].rearrange("p c w -> p (c w)"), "da0")
+        bank0 = sum_bank()
+        for h in range(2):
+            for cc in range(2):
+                mx(bank0[:, h * H:(h + 1) * H], xq0, x_cols(h, cc), daq0, slice(cc * H, (cc + 1) * H), cc == 0, cc == 1)
+
+        xq1 = quantize(x_turned[1][:].rearrange("p h w -> p (h w)"), "x1")
+        da_turned2 = keep.tile([P, C], BF16, name="da_turned2", align_bytes=64)
+        copy_turned(da_turned2[:], da_bank[2, 0][:])
+        daq2 = quantize(da_turned2[:], "da2")
 
         last = PASSES - 1
         acc = {}
         for ih in range(2):
             cols = slice(ih * P, (ih + 1) * P)
-            turned = keep.tile([P, P, PACK], BF16, name=f"da_turned{last}_{ih}", align_bytes=64)
+            turned = keep.tile([P, PASS], BF16, name=f"da_turned{last}_{ih}", align_bytes=64)
             copy_turned(turned[:], da_bank[last, ih][:, 2 * ih:2 * ih + 2, :])
-            piece = quantize(turned[:].rearrange("p w j -> p (w j)"), f"da{last}_{ih}")
+            piece = quantize(turned[:], f"da{last}_{ih}")
             acc[ih] = sum_bank()
             for h in range(2):
                 block = slice(h * P, (h + 1) * P)
-                mx(acc[ih][:, block], *x_block(h, last - 1), daq[last - 1], cols, True, False)
-                mx(acc[ih][:, block], *x_block(h, last), piece, slice(0, P), False, True)
+                mx(acc[ih][:, block], xq1, x_cols(h, 0), daq2, cols, True, False)
+                mx(acc[ih][:, block], xq1, x_cols(h, 1), piece, slice(0, P), False, True)
 
         res = keep.tile([P, 2, H], F32, name="res0")
         nc.scalar.copy(res[:].rearrange("p h i -> p (h i)"), bank0[:])

@@ -20,8 +20,13 @@ PACK = 4
 PASS = P * PACK
 PASSES = E * C // PASS
 LIST_COLS = PASS // 16
-X_BY_VECTOR = 512
-G32_BYTES = PACK * C * 4
+BANK_BYTES = 2048
+SLOTS = E * C
+BY_VECTOR = 1152
+G_BYTES = SLOTS * PACK * 2
+X_BANKS = ((0, 1), (5, 4))
+DH_BANKS = ((4, 5), (6, 7), (4, 0), (6, 1))
+DA_BANKS = (2, 3, 7, 2, 3)
 
 
 def tile_moe_mlp_relu_kernel(tc, xT, dyT, a, w2, gate, offs, out):
@@ -67,8 +72,8 @@ def tile_moe_mlp_relu_kernel(tc, xT, dyT, a, w2, gate, offs, out):
 
         for j in range(PACK):
             nc.sync.dma_start(dy[j][:], dy_rows[j])
-        load_w(0)
         load_x(0)
+        load_w(0)
         load_a(0)
         load_x(1)
         load_w(1)
@@ -88,29 +93,31 @@ def tile_moe_mlp_relu_kernel(tc, xT, dyT, a, w2, gate, offs, out):
         def half(c):
             return slice((c % 2) * PASS, (c % 2 + 1) * PASS)
 
-        def turned_bank():
-            return psum.tile([P, PACK, P], F32, name="turned", tag="turned", bufs=4)
+        def turned_bank(name, b):
+            return psum.tile([P, PACK, P], F32, name=name, offset=b * BANK_BYTES)
 
-        def sum_bank():
-            return psum.tile([P, PASS], F32, name="sums", tag="sums", bufs=4)
+        def sum_bank(name, b):
+            return psum.tile([P, PASS], F32, name=name, offset=b * BANK_BYTES)
 
-        gate_sb = [keep.tile([P, C], F32, name=f"gate_sb{e}", align_bytes=64) for e in range(E)]
+        gate_sb = keep.tile([P, SLOTS], F32, name="gate_sb", align_bytes=64)
         for e in range(E):
             copy = nc.vector.tensor_copy if e == 0 else nc.scalar.copy
             for b in range(2):
-                bank = turned_bank()
+                bank = turned_bank(f"gate{e}_{b}", 2 * e + b)
                 for i in range(PACK):
                     m = PACK * b + i
                     nc.tensor.transpose(bank[:, i, :], gate_cols[:, e, m:m + 1].to_broadcast([P, P]), ident[:])
-                copy(gate_sb[e][:].rearrange("q (p b i) -> q p b i", b=2, i=PACK)[:, :, b, :], bank[:].rearrange("q i p -> q p i"))
+                copy(gate_sb[:, e * C:(e + 1) * C].rearrange("q (p b i) -> q p b i", b=2, i=PACK)[:, :, b, :], bank[:].rearrange("q i p -> q p i"))
 
         def entries(lo, hi):
             return offsets[:, lo // 16:hi // 16]
 
-        g32 = [rows.tile([P, PACK, C], F32, name=f"g32_{e}", offset=e * G32_BYTES, align_bytes=64) for e in range(E)]
+        gated = keep.tile([P, PACK, BY_VECTOR], F32, name="gated", align_bytes=64)
+        plain = keep.tile([P, PACK, SLOTS - BY_VECTOR], F32, name="plain", align_bytes=64)
         for j in range(PACK):
-            nc.vector.tensor_tensor(g32[0][:, j, :], dy[j][:].indirect(entries(0, C)), gate_sb[0][:], ALU.mult)
-            nc.scalar.activation(g32[1][:, j, :], dy[j][:].indirect(entries(C, 2 * C)), COPY)
+            for lo, hi in ((0, C), (C, BY_VECTOR)) if j == 0 else ((0, BY_VECTOR),):
+                nc.vector.tensor_tensor(gated[:, j, lo:hi], dy[j][:].indirect(entries(lo, hi)), gate_sb[:, lo:hi], ALU.mult)
+            nc.scalar.activation(plain[:, j, :], dy[j][:].indirect(entries(BY_VECTOR, SLOTS)), COPY)
 
         def woven(dst):
             return dst.rearrange("p (c i) j -> p c j i", i=2)
@@ -129,36 +136,36 @@ def tile_moe_mlp_relu_kernel(tc, xT, dyT, a, w2, gate, offs, out):
             nc.scalar.copy(dst.bitcast(F32).rearrange("p (b r u) -> p b r u", r=P, u=2),
                            src.rearrange("p (b u) r -> p b r u", u=2))
 
-        w_bf0 = keep.tile([P, H, PACK], BF16, name="w_bf0", align_bytes=64)
-        nc.scalar.copy(woven(w_bf0[:]), planes(w_raw[0][:]))
+        g_bf = rows.tile([P, SLOTS, PACK], BF16, name="g_bf", offset=0, align_bytes=64)
+        gates = gate_sb[:, BY_VECTOR:].rearrange("p (c i) -> p c i", i=2).unsqueeze(2).to_broadcast([P, (SLOTS - BY_VECTOR) // 2, PACK, 2])
+        nc.vector.tensor_tensor(woven(g_bf[:, BY_VECTOR:, :]), planes(plain[:]), gates, ALU.mult)
+        nc.vector.tensor_copy(woven(g_bf[:, :BY_VECTOR, :]), planes(gated[:]))
 
-        g_bf = [keep.tile([P, C, PACK], BF16, name=f"g_bf{e}", align_bytes=64) for e in range(E)]
-        nc.vector.tensor_copy(woven(g_bf[0][:]), planes(g32[0][:]))
-
-        def gate_and_weave(c):
-            gates = gate_sb[1][:, half(c)].rearrange("p (c i) -> p c i", i=2).unsqueeze(2).to_broadcast([P, PASS // 2, PACK, 2])
-            nc.vector.tensor_tensor(woven(g_bf[1][:, half(c), :]), planes(g32[1][:, :, half(c)]), gates, ALU.mult)
-
-        x_slots = [keep.tile([P, E * C], BF16, name=f"x_slots{h}", align_bytes=64) for h in range(2)]
-        x_turned = [keep.tile([P, 2, C], BF16, name=f"x_turned{e}", align_bytes=64) for e in range(E)]
+        x_slots = {}
+        x_turned = [keep.tile([P, E, C], BF16, name=f"x_turned{h}", align_bytes=64) for h in range(2)]
         x_bank = {}
 
         def turn_x(h, lo, hi):
             for c in range(lo // PASS, hi // PASS):
                 if c % 2 == 0:
-                    x_bank[h, c // 2] = turned_bank()
+                    x_bank[h, c // 2] = turned_bank(f"x_bank{h}_{c}", X_BANKS[h][c // 2])
                 u = 2 * (c % 2)
-                turn_pairs(x_bank[h, c // 2][:, u:u + 2, :], x_slots[h][:, c * PASS:(c + 1) * PASS])
+                turn_pairs(x_bank[h, c // 2][:, u:u + 2, :], x_slots[h, c])
 
         def gather_x(h, lo, hi):
-            nc.scalar.activation(x_slots[h][:, lo:hi], x[h][:].indirect(entries(lo, hi)), COPY)
-            turn_x(h, lo, hi)
+            if (h, lo) in ((1, 0), (1, C + PASS)):
+                picked = rows.tile([P, hi - lo], BF16, name=f"x_slots{h}_{lo}", offset=G_BYTES, align_bytes=64)
+            else:
+                picked = keep.tile([P, hi - lo], BF16, name=f"x_slots{h}_{lo}", align_bytes=64)
+            for c in range(lo // PASS, hi // PASS):
+                x_slots[h, c] = picked[:, c * PASS - lo:(c + 1) * PASS - lo]
+            nc.scalar.activation(picked[:], x[h][:].indirect(entries(lo, hi)), COPY)
 
         def copy_x(h, e):
-            copy_turned(x_turned[e][:, h, :], x_bank[h, e][:])
+            copy_turned(x_turned[h][:, e, :], x_bank[h, e][:])
 
         def first_product(c, wq, gq):
-            banks = [sum_bank() for h in range(2)]
+            banks = [sum_bank(f"dh{c}_{h}", DH_BANKS[c][h]) for h in range(2)]
             for h in range(2):
                 mx(banks[h][:], wq, slice(h * P, (h + 1) * P), gq, half(c), True, True)
             return banks
@@ -167,55 +174,59 @@ def tile_moe_mlp_relu_kernel(tc, xT, dyT, a, w2, gate, offs, out):
 
         def mask_and_turn(c, dh):
             last = c == PASSES - 1
-            da_bank[c, 0] = turned_bank()
-            da_bank[c, 1] = turned_bank() if last else da_bank[c, 0]
+            da_bank[c, 0] = turned_bank(f"da_bank{c}", DA_BANKS[c])
+            da_bank[c, 1] = turned_bank(f"da_bank{c}_1", DA_BANKS[c + 1]) if last else da_bank[c, 0]
             da = keep.tile([P, 2, PASS], BF16, name=f"da{c}", align_bytes=64)
             for h in range(2):
                 nc.vector.scalar_tensor_tensor(da[:, h, :], a_sb[c // 2][:, h, half(c)], 0.0, dh[h][:],
                                                ALU.is_gt, ALU.mult)
                 turn_pairs(da_bank[c, h][:, 2 * h:2 * h + 2, :], da[:, h, :])
 
-        gate_and_weave(2)
-        gq0 = quantize(flat(g_bf[0]), "g0")
-        wq0 = quantize(flat(w_bf0), "w0")
         gather_x(0, 0, C)
-        gather_x(0, C, C + PASS)
-        gather_x(0, C + PASS, 2 * C)
+        turn_x(0, 0, C)
+        w_bf0 = keep.tile([P, H, PACK], BF16, name="w_bf0", align_bytes=64)
+        nc.scalar.copy(woven(w_bf0[:]), planes(w_raw[0][:]))
+        wq0 = quantize(flat(w_bf0), "w0")
+        gq0 = quantize(g_bf[:, :C, :].rearrange("p w j -> p (w j)"), "g0")
+        gq1 = quantize(g_bf[:, C:, :].rearrange("p w j -> p (w j)"), "g1")
+        for lo, hi in ((C, C + PASS), (C + PASS, 2 * C)):
+            gather_x(0, lo, hi)
+            turn_x(0, lo, hi)
         dh = {c: first_product(c, wq0, gq0) for c in range(2)}
-        gate_and_weave(3)
         copy_x(0, 0)
         copy_x(0, 1)
-        w_bf1 = rows.tile([P, H, PACK], BF16, name="w_bf1", offset=G32_BYTES, align_bytes=64)
+        w_bf1 = rows.tile([P, H, PACK], BF16, name="w_bf1", offset=0, align_bytes=64)
         nc.gpsimd.tensor_scalar(w_bf1[:], w_raw[1][:].rearrange("p j i -> p i j"), 1.0, 0.0, ALU.mult, ALU.add)
         gather_x(1, 0, C)
-        for c in range(2):
-            mask_and_turn(c, dh[c])
-        gather_x(1, C, 2 * C - X_BY_VECTOR)
-        gq1 = quantize(flat(g_bf[1]), "g1")
+        mask_and_turn(0, dh[0])
+        turn_x(1, 0, C)
+        mask_and_turn(1, dh[1])
+        gather_x(1, C, C + PASS)
         wq1 = quantize(flat(w_bf1), "w1")
         for c in range(2, PASSES):
             dh[c] = first_product(c, wq1, gq1)
-        nc.vector.tensor_copy(x_slots[1][:, 2 * C - X_BY_VECTOR:], x[1][:].indirect(entries(2 * C - X_BY_VECTOR, 2 * C)))
-        turn_x(1, 2 * C - X_BY_VECTOR, 2 * C)
+        xq = {0: quantize(x_turned[0][:].rearrange("p e w -> p (e w)"), "x0")}
         copy_x(1, 0)
+        xq[1, 0] = quantize(x_turned[1][:, 0, :], "x1_0")
+        gather_x(1, C + PASS, 2 * C)
         da_turned0 = keep.tile([P, 2, C], BF16, name="da_turned0", align_bytes=64)
         for c in range(2):
             copy_turned(da_turned0[:, c, :], da_bank[c, 0][:])
+        mask_and_turn(2, dh[2])
+        turn_x(1, C, 2 * C)
         copy_x(1, 1)
-        for c in range(2, PASSES):
-            mask_and_turn(c, dh[c])
+        mask_and_turn(3, dh[3])
 
-        def x_cols(h, cc):
-            return slice((2 * h + cc) * P, (2 * h + cc + 1) * P)
+        def x_block(h, c):
+            return (xq[0], slice(c * P, (c + 1) * P)) if h == 0 else (xq[1, c // 2], slice(c % 2 * P, (c % 2 + 1) * P))
 
-        xq0 = quantize(x_turned[0][:].rearrange("p h w -> p (h w)"), "x0")
         daq0 = quantize(da_turned0[:].rearrange("p c w -> p (c w)"), "da0")
-        bank0 = sum_bank()
+        bank0 = sum_bank("out0", 0)
         for h in range(2):
             for cc in range(2):
-                mx(bank0[:, h * H:(h + 1) * H], xq0, x_cols(h, cc), daq0, slice(cc * H, (cc + 1) * H), cc == 0, cc == 1)
+                mx(bank0[:, h * H:(h + 1) * H], *x_block(h, cc), daq0, slice(cc * H, (cc + 1) * H), cc == 0, cc == 1)
 
-        xq1 = quantize(x_turned[1][:].rearrange("p h w -> p (h w)"), "x1")
+        xq[1, 1] = quantize(x_turned[1][:, 1, :], "x1_1")
         da_turned2 = keep.tile([P, C], BF16, name="da_turned2", align_bytes=64)
         copy_turned(da_turned2[:], da_bank[2, 0][:])
         daq2 = quantize(da_turned2[:], "da2")
@@ -227,11 +238,11 @@ def tile_moe_mlp_relu_kernel(tc, xT, dyT, a, w2, gate, offs, out):
             turned = keep.tile([P, PASS], BF16, name=f"da_turned{last}_{ih}", align_bytes=64)
             copy_turned(turned[:], da_bank[last, ih][:, 2 * ih:2 * ih + 2, :])
             piece = quantize(turned[:], f"da{last}_{ih}")
-            acc[ih] = sum_bank()
+            acc[ih] = sum_bank(f"out1_{ih}", 6 - ih)
             for h in range(2):
                 block = slice(h * P, (h + 1) * P)
-                mx(acc[ih][:, block], xq1, x_cols(h, 0), daq2, cols, True, False)
-                mx(acc[ih][:, block], xq1, x_cols(h, 1), piece, slice(0, P), False, True)
+                mx(acc[ih][:, block], *x_block(h, last - 1), daq2, cols, True, False)
+                mx(acc[ih][:, block], *x_block(h, last), piece, slice(0, P), False, True)
 
         res = keep.tile([P, 2, H], F32, name="res0")
         nc.scalar.copy(res[:].rearrange("p h i -> p (h i)"), bank0[:])

@@ -19,14 +19,15 @@ P = 128
 PACK = 4
 PASS = P * PACK
 PASSES = E * C // PASS
-LIST_COLS = PASS // 16
 BANK_BYTES = 2048
 SLOTS = E * C
-BY_VECTOR = 1152
-G_BYTES = SLOTS * PACK * 2
-X_BANKS = ((0, 1), (5, 4))
-DH_BANKS = ((4, 5), (6, 7), (4, 0), (6, 1))
-DA_BANKS = (2, 3, 7, 2, 3)
+BY_GPSIMD = 448
+G_BYTES = C * PACK * 2
+GATE_BANKS = ((0, 1), (2, 3))
+X_BANKS = ((2, 3), (4, 2))
+DH_BANKS = ((4, 5), (6, 7), (2, 3), (5, 6))
+DA_BANKS = (0, 1, 7, 0, 1)
+OUT_BANKS = (4, 3, 5)
 
 
 def tile_moe_mlp_relu_kernel(tc, xT, dyT, a, w2, gate, offs, out):
@@ -74,8 +75,8 @@ def tile_moe_mlp_relu_kernel(tc, xT, dyT, a, w2, gate, offs, out):
             nc.sync.dma_start(dy[j][:], dy_rows[j])
         load_x(0)
         load_w(0)
-        load_a(0)
         load_x(1)
+        load_a(0)
         load_w(1)
         load_a(1)
 
@@ -99,25 +100,26 @@ def tile_moe_mlp_relu_kernel(tc, xT, dyT, a, w2, gate, offs, out):
         def sum_bank(name, b):
             return psum.tile([P, PASS], F32, name=name, offset=b * BANK_BYTES)
 
-        gate_sb = keep.tile([P, SLOTS], F32, name="gate_sb", align_bytes=64)
-        for e in range(E):
-            copy = nc.vector.tensor_copy if e == 0 else nc.scalar.copy
-            for b in range(2):
-                bank = turned_bank(f"gate{e}_{b}", 2 * e + b)
-                for i in range(PACK):
-                    m = PACK * b + i
-                    nc.tensor.transpose(bank[:, i, :], gate_cols[:, e, m:m + 1].to_broadcast([P, P]), ident[:])
-                copy(gate_sb[:, e * C:(e + 1) * C].rearrange("q (p b i) -> q p b i", b=2, i=PACK)[:, :, b, :], bank[:].rearrange("q i p -> q p i"))
+        def spread_gate(e, b):
+            bank = turned_bank(f"gate{e}_{b}", GATE_BANKS[e][b])
+            for i in range(PACK):
+                m = PACK * b + i
+                nc.tensor.transpose(bank[:, i, :], gate_cols[:, e, m:m + 1].to_broadcast([P, P]), ident[:])
+            return bank
+
+        gate_sb = keep.tile([P, C], F32, name="gate_sb", align_bytes=64)
+        for b, copy in enumerate((nc.vector.tensor_copy, nc.scalar.copy)):
+            copy(gate_sb[:].rearrange("q (p b i) -> q p b i", b=2, i=PACK)[:, :, b, :], spread_gate(1, b)[:].rearrange("q i p -> q p i"))
+        gate_bank = [spread_gate(0, b) for b in range(2)]
 
         def entries(lo, hi):
             return offsets[:, lo // 16:hi // 16]
 
-        gated = keep.tile([P, PACK, BY_VECTOR], F32, name="gated", align_bytes=64)
-        plain = keep.tile([P, PACK, SLOTS - BY_VECTOR], F32, name="plain", align_bytes=64)
+        gated = keep.tile([P, PACK, C], F32, name="gated", align_bytes=64)
+        plain = keep.tile([P, PACK, C], F32, name="plain", align_bytes=64)
         for j in range(PACK):
-            for lo, hi in ((0, C), (C, BY_VECTOR)) if j == 0 else ((0, BY_VECTOR),):
-                nc.vector.tensor_tensor(gated[:, j, lo:hi], dy[j][:].indirect(entries(lo, hi)), gate_sb[:, lo:hi], ALU.mult)
-            nc.scalar.activation(plain[:, j, :], dy[j][:].indirect(entries(BY_VECTOR, SLOTS)), COPY)
+            nc.vector.tensor_tensor(gated[:, j, :], dy[j][:].indirect(entries(C, SLOTS)), gate_sb[:], ALU.mult)
+            nc.scalar.activation(plain[:, j, :], dy[j][:].indirect(entries(0, C)), COPY)
 
         def woven(dst):
             return dst.rearrange("p (c i) j -> p c j i", i=2)
@@ -128,6 +130,9 @@ def tile_moe_mlp_relu_kernel(tc, xT, dyT, a, w2, gate, offs, out):
         def flat(tile):
             return tile[:].rearrange("p w j -> p (w j)")
 
+        def weave_on_gpsimd(dst, src):
+            nc.gpsimd.tensor_scalar(dst, src.rearrange("p j w -> p w j"), 1.0, 0.0, ALU.mult, ALU.add)
+
         def turn_pairs(dst, src):
             for u in range(2):
                 nc.tensor.transpose(dst[:, u, :], src.bitcast(F32)[:, u:PASS // 2:2], ident[:])
@@ -136,10 +141,17 @@ def tile_moe_mlp_relu_kernel(tc, xT, dyT, a, w2, gate, offs, out):
             nc.scalar.copy(dst.bitcast(F32).rearrange("p (b r u) -> p b r u", r=P, u=2),
                            src.rearrange("p (b u) r -> p b r u", u=2))
 
-        g_bf = rows.tile([P, SLOTS, PACK], BF16, name="g_bf", offset=0, align_bytes=64)
-        gates = gate_sb[:, BY_VECTOR:].rearrange("p (c i) -> p c i", i=2).unsqueeze(2).to_broadcast([P, (SLOTS - BY_VECTOR) // 2, PACK, 2])
-        nc.vector.tensor_tensor(woven(g_bf[:, BY_VECTOR:, :]), planes(plain[:]), gates, ALU.mult)
-        nc.vector.tensor_copy(woven(g_bf[:, :BY_VECTOR, :]), planes(gated[:]))
+        g_bf0 = keep.tile([P, C, PACK], BF16, name="g_bf0", align_bytes=64)
+        g_bf1 = rows.tile([P, C, PACK], BF16, name="g_bf1", offset=0, align_bytes=64)
+        for b in range(2):
+            nc.vector.tensor_tensor(
+                g_bf0[:].rearrange("q (p b i) j -> q b p j i", b=2, i=PACK)[:, b],
+                plain[:].rearrange("q j (p b i) -> q b p j i", b=2, i=PACK)[:, b],
+                gate_bank[b][:].rearrange("q i p -> q p i").unsqueeze(2).to_broadcast([P, P, PACK, PACK]), ALU.mult)
+        weave_on_gpsimd(g_bf1[:, :BY_GPSIMD, :], gated[:, :, :BY_GPSIMD])
+        w_bf0 = keep.tile([P, H, PACK], BF16, name="w_bf0", align_bytes=64)
+        weave_on_gpsimd(w_bf0[:], w_raw[0][:])
+        nc.vector.tensor_copy(woven(g_bf1[:, BY_GPSIMD:, :]), planes(gated[:, :, BY_GPSIMD:]))
 
         x_slots = {}
         x_turned = [keep.tile([P, E, C], BF16, name=f"x_turned{h}", align_bytes=64) for h in range(2)]
@@ -184,11 +196,9 @@ def tile_moe_mlp_relu_kernel(tc, xT, dyT, a, w2, gate, offs, out):
 
         gather_x(0, 0, C)
         turn_x(0, 0, C)
-        w_bf0 = keep.tile([P, H, PACK], BF16, name="w_bf0", align_bytes=64)
-        nc.scalar.copy(woven(w_bf0[:]), planes(w_raw[0][:]))
+        gq0 = quantize(flat(g_bf0), "g0")
         wq0 = quantize(flat(w_bf0), "w0")
-        gq0 = quantize(g_bf[:, :C, :].rearrange("p w j -> p (w j)"), "g0")
-        gq1 = quantize(g_bf[:, C:, :].rearrange("p w j -> p (w j)"), "g1")
+        gq1 = quantize(flat(g_bf1), "g1")
         for lo, hi in ((C, C + PASS), (C + PASS, 2 * C)):
             gather_x(0, lo, hi)
             turn_x(0, lo, hi)
@@ -196,7 +206,7 @@ def tile_moe_mlp_relu_kernel(tc, xT, dyT, a, w2, gate, offs, out):
         copy_x(0, 0)
         copy_x(0, 1)
         w_bf1 = rows.tile([P, H, PACK], BF16, name="w_bf1", offset=0, align_bytes=64)
-        nc.gpsimd.tensor_scalar(w_bf1[:], w_raw[1][:].rearrange("p j i -> p i j"), 1.0, 0.0, ALU.mult, ALU.add)
+        weave_on_gpsimd(w_bf1[:], w_raw[1][:])
         gather_x(1, 0, C)
         mask_and_turn(0, dh[0])
         turn_x(1, 0, C)
@@ -221,7 +231,7 @@ def tile_moe_mlp_relu_kernel(tc, xT, dyT, a, w2, gate, offs, out):
             return (xq[0], slice(c * P, (c + 1) * P)) if h == 0 else (xq[1, c // 2], slice(c % 2 * P, (c % 2 + 1) * P))
 
         daq0 = quantize(da_turned0[:].rearrange("p c w -> p (c w)"), "da0")
-        bank0 = sum_bank("out0", 0)
+        bank0 = sum_bank("out0", OUT_BANKS[0])
         for h in range(2):
             for cc in range(2):
                 mx(bank0[:, h * H:(h + 1) * H], *x_block(h, cc), daq0, slice(cc * H, (cc + 1) * H), cc == 0, cc == 1)
@@ -238,7 +248,7 @@ def tile_moe_mlp_relu_kernel(tc, xT, dyT, a, w2, gate, offs, out):
             turned = keep.tile([P, PASS], BF16, name=f"da_turned{last}_{ih}", align_bytes=64)
             copy_turned(turned[:], da_bank[last, ih][:, 2 * ih:2 * ih + 2, :])
             piece = quantize(turned[:], f"da{last}_{ih}")
-            acc[ih] = sum_bank(f"out1_{ih}", 6 - ih)
+            acc[ih] = sum_bank(f"out1_{ih}", OUT_BANKS[1 + ih])
             for h in range(2):
                 block = slice(h * P, (h + 1) * P)
                 mx(acc[ih][:, block], *x_block(h, last - 1), daq2, cols, True, False)

@@ -21,8 +21,10 @@ PASS = P * PACK
 PASSES = E * C // PASS
 BANK_BYTES = 2048
 SLOTS = E * C
-BY_GPSIMD = 448
+BY_GPSIMD = 512
+BY_SCALAR = 224
 G_BYTES = C * PACK * 2
+G0_AT = G_BYTES + 2 * C
 GATE_BANKS = ((0, 1), (2, 3))
 X_BANKS = ((2, 3), (4, 2))
 DH_BANKS = ((4, 5), (6, 7), (2, 3), (5, 6))
@@ -141,7 +143,7 @@ def tile_moe_mlp_relu_kernel(tc, xT, dyT, a, w2, gate, offs, out):
             nc.scalar.copy(dst.bitcast(F32).rearrange("p (b r u) -> p b r u", r=P, u=2),
                            src.rearrange("p (b u) r -> p b r u", u=2))
 
-        g_bf0 = keep.tile([P, C, PACK], BF16, name="g_bf0", align_bytes=64)
+        g_bf0 = rows.tile([P, C, PACK], BF16, name="g_bf0", offset=G0_AT, align_bytes=64)
         g_bf1 = rows.tile([P, C, PACK], BF16, name="g_bf1", offset=0, align_bytes=64)
         for b in range(2):
             nc.vector.tensor_tensor(
@@ -151,10 +153,13 @@ def tile_moe_mlp_relu_kernel(tc, xT, dyT, a, w2, gate, offs, out):
         weave_on_gpsimd(g_bf1[:, :BY_GPSIMD, :], gated[:, :, :BY_GPSIMD])
         w_bf0 = keep.tile([P, H, PACK], BF16, name="w_bf0", align_bytes=64)
         weave_on_gpsimd(w_bf0[:], w_raw[0][:])
-        nc.vector.tensor_copy(woven(g_bf1[:, BY_GPSIMD:, :]), planes(gated[:, :, BY_GPSIMD:]))
+        rest = BY_GPSIMD + BY_SCALAR
+        nc.scalar.copy(woven(g_bf1[:, BY_GPSIMD:rest, :]), planes(gated[:, :, BY_GPSIMD:rest]))
+        nc.vector.tensor_copy(woven(g_bf1[:, rest:, :]), planes(gated[:, :, rest:]))
 
         x_slots = {}
-        x_turned = [keep.tile([P, E, C], BF16, name=f"x_turned{h}", align_bytes=64) for h in range(2)]
+        x_turned = [rows.tile([P, E, C], BF16, name="x_turned0", offset=G0_AT, align_bytes=64),
+                    keep.tile([P, E, C], BF16, name="x_turned1", align_bytes=64)]
         x_bank = {}
 
         def turn_x(h, lo, hi):
@@ -203,8 +208,6 @@ def tile_moe_mlp_relu_kernel(tc, xT, dyT, a, w2, gate, offs, out):
             gather_x(0, lo, hi)
             turn_x(0, lo, hi)
         dh = {c: first_product(c, wq0, gq0) for c in range(2)}
-        copy_x(0, 0)
-        copy_x(0, 1)
         w_bf1 = rows.tile([P, H, PACK], BF16, name="w_bf1", offset=0, align_bytes=64)
         weave_on_gpsimd(w_bf1[:], w_raw[1][:])
         gather_x(1, 0, C)
@@ -212,6 +215,8 @@ def tile_moe_mlp_relu_kernel(tc, xT, dyT, a, w2, gate, offs, out):
         turn_x(1, 0, C)
         mask_and_turn(1, dh[1])
         gather_x(1, C, C + PASS)
+        copy_x(0, 0)
+        copy_x(0, 1)
         wq1 = quantize(flat(w_bf1), "w1")
         for c in range(2, PASSES):
             dh[c] = first_product(c, wq1, gq1)
@@ -242,27 +247,20 @@ def tile_moe_mlp_relu_kernel(tc, xT, dyT, a, w2, gate, offs, out):
         daq2 = quantize(da_turned2[:], "da2")
 
         last = PASSES - 1
-        acc = {}
+        acc = [sum_bank(f"out1_{h}", OUT_BANKS[1 + h]) for h in range(2)]
+        for h in range(2):
+            mx(acc[h][:, :H], *x_block(h, last - 1), daq2, slice(0, H), True, False)
         for ih in range(2):
-            cols = slice(ih * P, (ih + 1) * P)
             turned = keep.tile([P, PASS], BF16, name=f"da_turned{last}_{ih}", align_bytes=64)
             copy_turned(turned[:], da_bank[last, ih][:, 2 * ih:2 * ih + 2, :])
             piece = quantize(turned[:], f"da{last}_{ih}")
-            acc[ih] = sum_bank(f"out1_{ih}", OUT_BANKS[1 + ih])
             for h in range(2):
-                block = slice(h * P, (h + 1) * P)
-                mx(acc[ih][:, block], *x_block(h, last - 1), daq2, cols, True, False)
-                mx(acc[ih][:, block], *x_block(h, last), piece, slice(0, P), False, True)
+                mx(acc[h][:, ih * P:(ih + 1) * P], *x_block(h, last), piece, slice(0, P), False, ih == 1)
 
-        res = keep.tile([P, 2, H], F32, name="res0")
-        nc.scalar.copy(res[:].rearrange("p h i -> p (h i)"), bank0[:])
-        nc.sync.dma_start(out[0].rearrange("(h p) i -> p h i", p=P), res[:])
-        for ih in range(2):
-            cols = slice(ih * P, (ih + 1) * P)
-            res = keep.tile([P, 2, P], F32, name=f"res1_{ih}")
-            if ih == 0:
-                nc.vector.tensor_copy(res[:].rearrange("p h i -> p (h i)"), acc[ih][:, 0:2 * P])
-                nc.sync.dma_start(out[1].rearrange("(h p) i -> p h i", p=P)[:, :, cols], res[:])
-            else:
-                nc.scalar.copy(res[:].rearrange("p h i -> p (h i)"), acc[ih][:, 0:2 * P])
-                nc.scalar.dma_start(out[1].rearrange("(h p) i -> p h i", p=P)[:, :, cols], res[:])
+        res0 = keep.tile([P, 2, H], F32, name="res0")
+        nc.scalar.copy(res0[:].rearrange("p h i -> p (h i)"), bank0[:])
+        nc.sync.dma_start(out[0].rearrange("(h p) i -> p h i", p=P), res0[:])
+        for h, (copy, queue) in enumerate(((nc.vector.tensor_copy, nc.sync), (nc.scalar.copy, nc.scalar))):
+            res = keep.tile([P, H], F32, name=f"res1_{h}")
+            copy(res[:], acc[h][:, :H])
+            queue.dma_start(out[1, h * P:(h + 1) * P, :], res[:])

@@ -22,7 +22,7 @@ PASSES = E * C // PASS
 BANK_BYTES = 2048
 SLOTS = E * C
 BY_GPSIMD = 512
-BY_SCALAR = 224
+BY_SCALAR = 128
 G_BYTES = C * PACK * 2
 G0_AT = G_BYTES + 2 * C
 GATE_BANKS = ((0, 1), (2, 3))

from contextlib import ExitStack

import concourse.mybir as mybir

K, T, E, C, H, N = 256, 2560, 2, 1024, 256, 512
FLOPS = 2 * E * C * (N * H + K * H)
BYTES = 4 * (K * T + N * T + H * E * C + E * N * H + E * C + E * K * H) + 2 * 128 * 128

F32 = mybir.dt.float32
BF16 = mybir.dt.bfloat16
U32 = mybir.dt.uint32
U16 = mybir.dt.uint16
U8 = mybir.dt.uint8
FP8X4 = mybir.dt.float8_e4m3fn_x4
ALU = mybir.AluOpType
COPY = mybir.ActivationFunctionType.Copy

P = 128
PACK = 4
PASS = P * PACK
PASSES = E * C // PASS
BANK_BYTES = 2048
SLOTS = E * C
BY_GPSIMD = 512
BY_SCALAR = 128
G_BYTES = C * PACK * 2
G0_AT = G_BYTES + 2 * C
GATE_BANKS = ((0, 1), (2, 3))
X_BANKS = ((2, 3), (4, 2))
DH_BANKS = ((4, 5), (6, 7), (2, 3), (5, 6))
DA_BANKS = (0, 1, 7, 0, 1)
OUT_BANKS = (4, 3, 5)


def tile_moe_mlp_relu_kernel(tc, xT, dyT, a, w2, gate, offs, out):
    nc = tc.nc
    with ExitStack() as ctx:
        keep = ctx.enter_context(tc.tile_pool(name="keep", bufs=1))
        rows = ctx.enter_context(tc.tile_pool(name="rows", bufs=1))
        psum = ctx.enter_context(tc.psum_pool(name="psum", bufs=1))

        offsets = keep.tile([P, E * C // 16], U16, name="offsets")

        gate_cols = keep.tile([P, E, 2 * PACK], F32, name="gate_cols")
        nc.sync.dma_start(gate_cols[:], gate[0, :].rearrange("(e p m) -> p e m", e=E, p=P))
        nc.sync.dma_start(offsets[:], offs)

        ident = keep.tile([P, P], F32, name="ident")
        ones = keep.tile([P, 32], F32, name="ones")
        count = keep.tile([P, 32], F32, name="count", align_bytes=64)
        count_t = keep.tile([P, 32], F32, name="count_t", align_bytes=64)
        nc.vector.memset(ones[:], 1.0)
        nc.vector.memset(ident[:], 0.0)
        nc.vector.tensor_tensor_scan(count[:], ones[:], ones[:], 0.0, ALU.mult, ALU.add)
        nc.vector.transpose(count_t[:], count[:])
        for q in range(4):
            quad = slice(32 * q, 32 * q + 32)
            nc.vector.tensor_tensor(ident[quad, quad], count[quad, :], count_t[quad, :], ALU.is_equal)

        dy_rows = dyT.rearrange("(p j) t -> j p t", j=PACK)
        dy = [keep.tile([P, T], F32, name=f"dy{j}", align_bytes=64) for j in range(PACK)]
        x = [keep.tile([P, T], F32, name=f"x{h}", align_bytes=64) for h in range(2)]
        w_raw = [keep.tile([P, PACK, H], F32, name=f"w_raw{e}") for e in range(E)]
        a_rows = a.rearrange("(h p) s -> p h s", p=P)
        a_sb = [keep.tile([P, 2, C], F32, name=f"a_sb{e}") for e in range(E)]

        def load_x(h):
            nc.sync.dma_start(x[h][:], xT[h * P:(h + 1) * P, :])

        def load_w(e):
            nc.sync.dma_start(w_raw[e][:], w2[e].rearrange("(p j) i -> p j i", j=PACK))

        def load_a(e):
            nc.sync.dma_start(a_sb[e][:], a_rows[:, :, e * C:(e + 1) * C])

        for j in range(PACK):
            nc.sync.dma_start(dy[j][:], dy_rows[j])
        load_x(0)
        load_w(0)
        load_x(1)
        load_a(0)
        load_w(1)
        load_a(1)

        def quantize(src, name):
            width = src.shape[1] // PACK
            codes = keep.tile([P, width], U32, name=name + "_codes", align_bytes=64)
            scales = keep.tile([P, width], U8, name=name + "_scales", align_bytes=64)
            nc.vector.quantize_mx(out=codes[:].bitcast(FP8X4), scales=scales[:], in_=src)
            return codes, scales

        def mx(dst, lhs, lhs_cols, rhs, rhs_cols, start, stop):
            nc.tensor.matmul_mx(dst, lhsT=lhs[0][:, lhs_cols].bitcast(FP8X4), lhsT_scale=lhs[1][:, lhs_cols],
                                rhs=rhs[0][:, rhs_cols].bitcast(FP8X4), rhs_scale=rhs[1][:, rhs_cols], start=start, stop=stop)

        def half(c):
            return slice((c % 2) * PASS, (c % 2 + 1) * PASS)

        def turned_bank(name, b):
            return psum.tile([P, PACK, P], F32, name=name, offset=b * BANK_BYTES)

        def sum_bank(name, b):
            return psum.tile([P, PASS], F32, name=name, offset=b * BANK_BYTES)

        def spread_gate(e, b):
            bank = turned_bank(f"gate{e}_{b}", GATE_BANKS[e][b])
            for i in range(PACK):
                m = PACK * b + i
                nc.tensor.transpose(bank[:, i, :], gate_cols[:, e, m:m + 1].to_broadcast([P, P]), ident[:])
            return bank

        gate_sb = keep.tile([P, C], F32, name="gate_sb", align_bytes=64)
        for b, copy in enumerate((nc.vector.tensor_copy, nc.scalar.copy)):
            copy(gate_sb[:].rearrange("q (p b i) -> q p b i", b=2, i=PACK)[:, :, b, :], spread_gate(1, b)[:].rearrange("q i p -> q p i"))
        gate_bank = [spread_gate(0, b) for b in range(2)]

        def entries(lo, hi):
            return offsets[:, lo // 16:hi // 16]

        gated = keep.tile([P, PACK, C], F32, name="gated", align_bytes=64)
        plain = keep.tile([P, PACK, C], F32, name="plain", align_bytes=64)
        for j in range(PACK):
            nc.vector.tensor_tensor(gated[:, j, :], dy[j][:].indirect(entries(C, SLOTS)), gate_sb[:], ALU.mult)
            nc.scalar.activation(plain[:, j, :], dy[j][:].indirect(entries(0, C)), COPY)

        def woven(dst):
            return dst.rearrange("p (c i) j -> p c j i", i=2)

        def planes(src):
            return src.rearrange("p j (c i) -> p c j i", i=2)

        def flat(tile):
            return tile[:].rearrange("p w j -> p (w j)")

        def weave_on_gpsimd(dst, src):
            nc.gpsimd.tensor_scalar(dst, src.rearrange("p j w -> p w j"), 1.0, 0.0, ALU.mult, ALU.add)

        def turn_pairs(dst, src):
            for u in range(2):
                nc.tensor.transpose(dst[:, u, :], src.bitcast(F32)[:, u:PASS // 2:2], ident[:])

        def copy_turned(dst, src):
            nc.scalar.copy(dst.bitcast(F32).rearrange("p (b r u) -> p b r u", r=P, u=2),
                           src.rearrange("p (b u) r -> p b r u", u=2))

        g_bf0 = rows.tile([P, C, PACK], BF16, name="g_bf0", offset=G0_AT, align_bytes=64)
        g_bf1 = rows.tile([P, C, PACK], BF16, name="g_bf1", offset=0, align_bytes=64)
        for b in range(2):
            nc.vector.tensor_tensor(
                g_bf0[:].rearrange("q (p b i) j -> q b p j i", b=2, i=PACK)[:, b],
                plain[:].rearrange("q j (p b i) -> q b p j i", b=2, i=PACK)[:, b],
                gate_bank[b][:].rearrange("q i p -> q p i").unsqueeze(2).to_broadcast([P, P, PACK, PACK]), ALU.mult)
        weave_on_gpsimd(g_bf1[:, :BY_GPSIMD, :], gated[:, :, :BY_GPSIMD])
        w_bf0 = keep.tile([P, H, PACK], BF16, name="w_bf0", align_bytes=64)
        weave_on_gpsimd(w_bf0[:], w_raw[0][:])
        rest = BY_GPSIMD + BY_SCALAR
        nc.scalar.copy(woven(g_bf1[:, BY_GPSIMD:rest, :]), planes(gated[:, :, BY_GPSIMD:rest]))
        nc.vector.tensor_copy(woven(g_bf1[:, rest:, :]), planes(gated[:, :, rest:]))

        x_slots = {}
        x_turned = [rows.tile([P, E, C], BF16, name="x_turned0", offset=G0_AT, align_bytes=64),
                    keep.tile([P, E, C], BF16, name="x_turned1", align_bytes=64)]
        x_bank = {}

        def turn_x(h, lo, hi):
            for c in range(lo // PASS, hi // PASS):
                if c % 2 == 0:
                    x_bank[h, c // 2] = turned_bank(f"x_bank{h}_{c}", X_BANKS[h][c // 2])
                u = 2 * (c % 2)
                turn_pairs(x_bank[h, c // 2][:, u:u + 2, :], x_slots[h, c])

        def gather_x(h, lo, hi):
            if (h, lo) in ((1, 0), (1, C + PASS)):
                picked = rows.tile([P, hi - lo], BF16, name=f"x_slots{h}_{lo}", offset=G_BYTES, align_bytes=64)
            else:
                picked = keep.tile([P, hi - lo], BF16, name=f"x_slots{h}_{lo}", align_bytes=64)
            for c in range(lo // PASS, hi // PASS):
                x_slots[h, c] = picked[:, c * PASS - lo:(c + 1) * PASS - lo]
            nc.scalar.activation(picked[:], x[h][:].indirect(entries(lo, hi)), COPY)

        def copy_x(h, e):
            copy_turned(x_turned[h][:, e, :], x_bank[h, e][:])

        def first_product(c, wq, gq):
            banks = [sum_bank(f"dh{c}_{h}", DH_BANKS[c][h]) for h in range(2)]
            for h in range(2):
                mx(banks[h][:], wq, slice(h * P, (h + 1) * P), gq, half(c), True, True)
            return banks

        da_bank = {}

        def mask_and_turn(c, dh):
            last = c == PASSES - 1
            da_bank[c, 0] = turned_bank(f"da_bank{c}", DA_BANKS[c])
            da_bank[c, 1] = turned_bank(f"da_bank{c}_1", DA_BANKS[c + 1]) if last else da_bank[c, 0]
            da = keep.tile([P, 2, PASS], BF16, name=f"da{c}", align_bytes=64)
            for h in range(2):
                nc.vector.scalar_tensor_tensor(da[:, h, :], a_sb[c // 2][:, h, half(c)], 0.0, dh[h][:],
                                               ALU.is_gt, ALU.mult)
                turn_pairs(da_bank[c, h][:, 2 * h:2 * h + 2, :], da[:, h, :])

        gather_x(0, 0, C)
        turn_x(0, 0, C)
        gq0 = quantize(flat(g_bf0), "g0")
        wq0 = quantize(flat(w_bf0), "w0")
        gq1 = quantize(flat(g_bf1), "g1")
        for lo, hi in ((C, C + PASS), (C + PASS, 2 * C)):
            gather_x(0, lo, hi)
            turn_x(0, lo, hi)
        dh = {c: first_product(c, wq0, gq0) for c in range(2)}
        w_bf1 = rows.tile([P, H, PACK], BF16, name="w_bf1", offset=0, align_bytes=64)
        weave_on_gpsimd(w_bf1[:], w_raw[1][:])
        gather_x(1, 0, C)
        mask_and_turn(0, dh[0])
        turn_x(1, 0, C)
        mask_and_turn(1, dh[1])
        gather_x(1, C, C + PASS)
        copy_x(0, 0)
        copy_x(0, 1)
        wq1 = quantize(flat(w_bf1), "w1")
        for c in range(2, PASSES):
            dh[c] = first_product(c, wq1, gq1)
        xq = {0: quantize(x_turned[0][:].rearrange("p e w -> p (e w)"), "x0")}
        copy_x(1, 0)
        xq[1, 0] = quantize(x_turned[1][:, 0, :], "x1_0")
        gather_x(1, C + PASS, 2 * C)
        da_turned0 = keep.tile([P, 2, C], BF16, name="da_turned0", align_bytes=64)
        for c in range(2):
            copy_turned(da_turned0[:, c, :], da_bank[c, 0][:])
        mask_and_turn(2, dh[2])
        turn_x(1, C, 2 * C)
        copy_x(1, 1)
        mask_and_turn(3, dh[3])

        def x_block(h, c):
            return (xq[0], slice(c * P, (c + 1) * P)) if h == 0 else (xq[1, c // 2], slice(c % 2 * P, (c % 2 + 1) * P))

        daq0 = quantize(da_turned0[:].rearrange("p c w -> p (c w)"), "da0")
        bank0 = sum_bank("out0", OUT_BANKS[0])
        for h in range(2):
            for cc in range(2):
                mx(bank0[:, h * H:(h + 1) * H], *x_block(h, cc), daq0, slice(cc * H, (cc + 1) * H), cc == 0, cc == 1)

        xq[1, 1] = quantize(x_turned[1][:, 1, :], "x1_1")
        da_turned2 = keep.tile([P, C], BF16, name="da_turned2", align_bytes=64)
        copy_turned(da_turned2[:], da_bank[2, 0][:])
        daq2 = quantize(da_turned2[:], "da2")

        last = PASSES - 1
        acc = [sum_bank(f"out1_{h}", OUT_BANKS[1 + h]) for h in range(2)]
        for h in range(2):
            mx(acc[h][:, :H], *x_block(h, last - 1), daq2, slice(0, H), True, False)
        for ih in range(2):
            turned = keep.tile([P, PASS], BF16, name=f"da_turned{last}_{ih}", align_bytes=64)
            copy_turned(turned[:], da_bank[last, ih][:, 2 * ih:2 * ih + 2, :])
            piece = quantize(turned[:], f"da{last}_{ih}")
            for h in range(2):
                mx(acc[h][:, ih * P:(ih + 1) * P], *x_block(h, last), piece, slice(0, P), False, ih == 1)

        res0 = keep.tile([P, 2, H], F32, name="res0")
        nc.scalar.copy(res0[:].rearrange("p h i -> p (h i)"), bank0[:])
        nc.sync.dma_start(out[0].rearrange("(h p) i -> p h i", p=P), res0[:])
        for h, (copy, queue) in enumerate(((nc.vector.tensor_copy, nc.sync), (nc.scalar.copy, nc.scalar))):
            res = keep.tile([P, H], F32, name=f"res1_{h}")
            copy(res[:], acc[h][:, :H])
            queue.dma_start(out[1, h * P:(h + 1) * P, :], res[:])
